import numpy as np, ml_dtypes
CORES = [66,74,82,90,194,202,210,218]
N = 8
import mx_ref
BF = ml_dtypes.bfloat16
def entries(a):
    return np.ascontiguousarray(a.T).reshape(-1)
def table(e):
    return np.ascontiguousarray(np.reshape(e, (-1, 16)).T).astype(np.int32)
def pick(q, e):
    c = np.concatenate([q[0].reshape(128, -1, 4), np.zeros((128, 1, 4), np.uint8)], axis=1); s = np.concatenate([q[1], np.ones((16, 1), np.uint8)], axis=1)
    return (np.ascontiguousarray(c[:, e].reshape(128, -1)), np.ascontiguousarray(s[:, e]))
def join(*qs):
    return (np.concatenate([q[0] for q in qs], axis=1), np.concatenate([q[1] for q in qs], axis=1))
def put(q, e, v):
    c, s = q[0].reshape(128, -1, 4).copy(), q[1].copy(); c[:, e] = v[0].reshape(128, -1, 4); s[:, e] = v[1]
    return (c.reshape(128, -1), s)
def pk(c, s):
    return (np.ascontiguousarray(c), mx_ref.live(s))
def emit(q):
    return q[0], q[1]
def packed(v, rng):
    q = [mx_ref.quantize(np.ascontiguousarray(v[r])) for r in range(N)]
    return np.stack([a for a, b in q]), np.stack([mx_ref.plane(b, rng) for a, b in q])
def f(rng, *shape):
    return mx_ref.flush((rng.standard_normal(shape, dtype=np.float32) * np.exp2(rng.integers(-2, 3, shape[:-1] + (1,)))).astype(BF))
def wide(rng, *shape, cols=0):
    v = rng.standard_normal(shape, dtype=np.float32) * np.exp2(rng.integers(-12, 13, shape)).astype(np.float32)
    if cols: v *= np.repeat(np.exp2(rng.integers(-cols, cols + 1, shape[:-2] + (1, shape[-1] // 4))) * (rng.random(shape[:-2] + (1, shape[-1] // 4)) > 0.0625), 4, axis=-1).astype(np.float32)
    return mx_ref.flush(v.astype(BF))
C, CB, CAPP, S = 256, 80, 48, 288
def counts(rng, total, cap, least):
    n = np.array(least)
    while n.sum() < total: n[rng.choice(np.flatnonzero(n < cap))] += 1
    return n
def runs(rng, least, cap):
    n = np.zeros((N, N), int)
    for s in range(N)[::-1]: n[s] = counts(rng, C, np.minimum(cap[s], CAPP + n[N - 1]), least[s])
    return n
def keeps(rng, n, fall=0, least=np.zeros((N, N), int)):
    k = np.zeros((N, N), int)
    for s in range(N)[::-1]:
        above = k.sum(axis=0)
        k[s] = np.clip(np.minimum(rng.integers(0, 2 * n[s] // 3 + 1), n[s] - fall), np.maximum(n[s] - above, least[s]), np.minimum(np.minimum(n[s], CAPP), S - above))
    return k
def lists(rng, n, k, ends=False, narrow=False):
    p = np.sort(rng.choice(65536 - 2 * N * S, N - 1, replace=False)) + 2 * S * np.arange(1, N)
    if ends: p[0] = int(k[:, 0].sum()) + 2 + int(rng.integers(0, 4))
    if narrow: p[-1] = 65535
    lo, hi = np.append(0, p), np.append(p, 65536)
    keys = [[] for s in range(N)]
    for d in range(N):
        e, i, j = int(ends), -1, -1
        u = lo[d] + e + rng.choice(int(hi[d] - lo[d]) - 2 * e, int(k[:, d].sum()), replace=False)
        at = np.append(np.cumsum(k[::-1, d])[::-1], 0)[1:]
        if ends:
            low, c = np.flatnonzero(n[:, d] - k[:, d] > 1), np.flatnonzero(k[:, d] > 1)
            c = c[c > low[0]]
            if d in (0, N - 1): c = c[c < N - 1]
            i = rng.choice(c); j = rng.choice(low[low < i])
            u[at[i]] = lo[d]; u[at[i] + 1] = hi[d] - 1
        for s in range(N):
            m = at[i] + np.arange(2) if s == j else np.zeros(0, int)
            old = np.concatenate([m, rng.permutation(np.setdiff1d(np.arange(at[s]), m))])[:n[s, d] - k[s, d]]
            keys[s].append(u[np.concatenate([old, at[s] + np.arange(k[s, d])])])
    return {"ky": np.stack([table(np.sort(np.concatenate(v))) for v in keys]), "sp": np.stack([table(np.append(p, np.full(17 - N, 65535)))] * N)}
def setup_inputs(rng):
    kc, ks = packed(f(rng, N, 128, 4 * C), rng)
    n = runs(rng, rng.integers(1, CAPP // 2 + 1, (N, N)), np.full((N, N), CB))
    return {"kc": kc, "ks": ks, "w": f(rng, N, 128, 512), **lists(rng, n, keeps(rng, n))}
def setup_inputs_single(rng):
    least, cap = rng.integers(1, CAPP // 2 + 1, (N, N)), np.full((N, N), CB)
    least[:, N - 1] = rng.integers(0, 2, N); least[rng.permutation(N - 1)[:2], N - 1] = 1; cap[:, N - 1] = least[:, N - 1]
    n = runs(rng, least, cap)
    return {**setup_inputs(rng), **lists(rng, n, keeps(rng, n), narrow=True)}
def setup_inputs_narrow(rng):
    least, cap = rng.integers(1, CAPP // 2 + 1, (N, N)), np.full((N, N), CB)
    least[:, N - 1] = 0; cap[:, N - 1] = 0
    n = runs(rng, least, cap)
    return {**setup_inputs(rng), **lists(rng, n, keeps(rng, n), narrow=True)}
def setup_inputs_full(rng):
    h = int(rng.integers(0, N)); least = np.ones((N, N), int)
    a = np.append(h, rng.permutation(np.delete(np.arange(N), h)))[:(C - N) // CAPP]
    least[N - 1, a] = CAPP
    for s in range(N - 1): least[s, np.append(h, rng.permutation(a[1:]))[:(C - N) // CB]] = CB
    n = runs(rng, least, np.full((N, N), CB)); k = keeps(rng, n)
    v = np.zeros(N, int); v[N - 2:] = CAPP; v[rng.permutation(N - 2)[:S // CAPP - 2]] = CAPP
    k[:, h] = counts(rng, S, CAPP, v)
    return {**setup_inputs(rng), **lists(rng, n, k)}
def setup_inputs_edges(rng):
    q = int(rng.integers(1, N)); h = int(rng.choice(np.delete(np.arange(N - 1), min(q, N - 2))))
    least, cap = rng.integers(2, CAPP // 2 + 1, (N, N)), np.full((N, N), CB)
    least[h, q] = 0; cap[h, q] = 0
    few = rng.integers(2, 5, N)
    few[rng.permutation(np.setdiff1d(np.arange(N), [int(rng.integers(0, N - 2)), N - 2]))[:int(rng.integers(2, N - 1))]] = 0
    least[:, 0] = few; cap[:, 0] = few
    n = runs(rng, least, cap)
    two = np.zeros((N, N), int); two[N - 2, [0, N - 1]] = 2
    return {**setup_inputs(rng), **lists(rng, n, keeps(rng, n, 2, two), ends=True)}
def setup_inputs_spread(rng):
    d = setup_inputs(rng); d["kc"], d["ks"] = packed(wide(rng, N, 128, 4 * C, cols=8), rng); return d
def check_inputs(d):
    b = []
    p = entries(d["sp"][0]).astype(np.int64); g = p[:N - 1]
    if (d["sp"] != d["sp"][:1]).any() or (p[N - 1:] != 65535).any() or g.min() < 1 or g.max() > 65535 or (np.diff(g) <= 0).any(): b.append("sp")
    lo, hi = np.append(0, g), np.append(g, 65536)
    k = [entries(d["ky"][s]).astype(np.int64) for s in range(N)]
    bad = any(v.min() < 0 or v.max() > 65535 or (np.diff(v) <= 0).any() for v in k)
    x, s = np.concatenate(k), np.repeat(np.arange(N), C)
    o = np.argsort(x, kind="stable"); o = o[np.append(x[o][1:] != x[o][:-1], True)]
    x, s = x[o], s[o]
    for q in range(N):
        m = (x >= lo[q]) & (x < hi[q])
        if max(((v >= lo[q]) & (v < hi[q])).sum() for v in k) > CB or m.sum() > S or np.bincount(s[m], minlength=N).max() > CAPP: bad = True
    if bad: b.append("ky")
    return b
def reference(kc, ks, w, ky, sp):
    every = join(*[pk(kc[s], ks[s]) for s in range(N)])
    keys = np.concatenate([entries(ky[s]) for s in range(N)])
    oc, osc = np.zeros((N, 128, 4 * S), np.uint8), np.zeros((N, 16, S), np.uint8)
    ok, y = np.zeros((N, 2, S), np.float32), np.zeros((N, 128, S), np.float32)
    for d in range(N):
        p = entries(sp[d])[:N - 1]
        lo, hi = np.append(0, p)[d], np.append(p, 65536)[d]
        e = np.flatnonzero((keys >= lo) & (keys < hi))
        e = e[np.argsort(keys[e], kind="stable")]
        e = e[np.append(keys[e][1:] != keys[e][:-1], True)[:e.size]]
        a = np.full(S, -1); a[:e.size] = e
        kept = pick(every, a)
        oc[d], osc[d] = emit(kept)
        ok[d, 0] = np.where(a >= 0, keys[a], -1); ok[d, 1] = np.where(a >= 0, a // C, -1)
        y[d] = mx_ref.matmul(mx_ref.quantize(np.ascontiguousarray(w[d])), kept)
    return {"oc": oc, "osc": osc, "ok": ok, "y": y}

@@ -1,0 +1,315 @@
+from concourse.bass import DstId, RemoteDMATransfer
+from concourse.mybir import dt, AluOpType as A, AxisListType, ActivationFunctionType as AF
+
+N, C, CAPP, S = 8, 256, 48, 288
+SLOTS = N * CAPP
+ZC = SLOTS // 2
+ZE = ZC + 16
+FIN = SLOTS + 16
+
+
+def at(s):
+    return CAPP * s + (16 if CAPP * s >= ZC else 0)
+
+
+F32, BF, I32, U16, CODE, U8 = "float32", "bfloat16", "int32", "uint16", "float8_e4m3fn_x4", "uint8"
+SCRATCH = {
+    "land": ("dram", [N, 128, 2], I32),
+    "land3": ("dram", [N, 128, 6], U16),
+    "f1": ("sbuf", [64, 16], F32), "f2": ("sbuf", [32, 16], F32),
+    "g1": ("sbuf", [64, 36], F32), "g2": ("sbuf", [32, 36], F32), "g3": ("sbuf", [32, 18], F32),
+    "acc": ("psum", [128, 1024], F32),
+}
+for _d, _l in ((I32, "lk 16, owni 16, spi 16, spb 16, pidx 1, q16 1, blk 1, half 1, il8 16, il16 32, idg 32, hi 3"),
+               (U16, "lku 16, ownu 16, e8 16, eh 16, e16 32, edg 32, wl 24, m6 6, ix 8, ou 6, ol 18"),
+               (BF, "win 65536, ones 256, vals 256, vals2 96, hb 256, xt 256, f3 8, ex 256, lin 256, junk 1024, cmp 514, zt 512, "
+                    "wt 512, junk2 800, cmp2 402, L 2400, LT 576"),
+               (F32, "lkf 16, ownf 16, spf 16, q16f 1, halff 1, b96 1, c1 1, c2 1, c3 1, c4 1, c5 1, it6 6, bt 6, tt6 6, itr 3, "
+                     "trash 3, iv 96, rk 400, tmp 128, tmpb 64, tmpc 32, basew 16, baseb 256, base 256, num 256, cnt 6, wf 24, "
+                     "kx 512, kg 512, kl 544, k96 96, kt 96, kf 400, inv 3, tr 3, s2 3, pos 3, h16 3, h32 3, okk 288, okr 288, "
+                     "yfin 400, ysb 288"),
+               (CODE, "kown 272, slot 384, fin 400, ord 288, wq 128, zq 128"),
+               (U8, "kowns 272, slots 384, fins 400, ords 288, wqs 128, zqs 128")):
+    for _e in _l.split(", "):
+        SCRATCH[_e.split(" ")[0]] = ("sbuf", [128, int(_e.split(" ")[1])], _d)
+SEMAPHORES = ["v", "s", "gc1", "gc2", "gc3", "mm", "lland", "lown", "lsp", "lk", "lw", "larr", "lmsg", "lix", "lfin", "lzero",
+              "st", "akey", "acode", "ascale", "amsg", "xkey", "xcode", "xscale", "xmsg"]
+
+
+def rank_program(g, core, T, topo):
+    r = T.rank_of(core)
+    if r is None:
+        return
+    M = T.sem
+    others = [d for d in range(N) if d != r]
+    n = {"v": 0, "s": 0}
+
+    def V(call, *a, dep=True):
+        if dep and n["v"]:
+            g.vector.wait_ge(M.v, n["v"])
+        call(*a).then_inc(M.v, 1)
+        n["v"] += 1
+
+    def act(*a, dep=True, **k):
+        if dep and n["s"]:
+            g.scalar.wait_ge(M.s, n["s"])
+        g.scalar.activation(*a, **k).then_inc(M.s, 1)
+        n["s"] += 1
+
+    tc, tt, ts = g.vector.tensor_copy, g.vector.tensor_tensor, g.vector.tensor_scalar
+    ms, tp, red = g.vector.memset, g.vector.transpose, g.vector.tensor_reduce
+
+    def dst(d):
+        rid, pid = topo.addr(T.cores[d], core)
+        return DstId(rid=rid, pnc=pid)
+
+    def eng(d, k):
+        return 1 << topo.engines(core, T.cores[d])[k]
+
+    def iota(sem, out, pattern, base, f=True):
+        if f:
+            g.iota(out, pattern, base, 0, allow_small_or_imprecise_dtypes=True).then_inc(sem, 1)
+        else:
+            g.iota(out, pattern, base, 0).then_inc(sem, 1)
+
+    g.sync.dma_start(T.land[r], T.ky[:]).then_inc(M.lland, 16)
+    for h in range(2):
+        g.scalar.dma_start(T.owni[16 * h:16 * h + 16, :], T.ky[:]).then_inc(M.lown, 16)
+    g.sync.dma_start(T.spi[0:1, :], T.sp[:]).then_inc(M.lsp, 16)
+    for a, b in ((0, C), (C, 272)):
+        g.scalar.dma_start(T.kown[:, a:b].bitcast(dt.uint8), T.kc[:, 0:4 * (b - a)]).then_inc(M.lk, 16)
+        g.scalar.dma_start(T.kowns[:, a:b], T.ks[:, 0:b - a]).then_inc(M.lk, 16)
+    g.scalar.dma_start(T.wt[:], T.w[:]).then_inc(M.lw, 16)
+
+    g.iota(T.pidx[:], [[0, 1]], 0, 1).then_inc(M.gc1, 1)
+    iota(M.gc1, T.il8[:], [[1, 8], [0, 2]], 0, False)
+    iota(M.gc1, T.it6[:], [[16, 6]], 0)
+    g.wait_ge(M.lland, 16)
+    g.remote_dma_fused([RemoteDMATransfer(dst_ids=[dst(d)], dma_engine_mask=eng(d, k), remote_sem=M.akey,
+                                          src=T.land[r], dst=T.land[r]) for k, d in enumerate(others)], local_sem=M.xkey)
+    V(ms, T.ones[:], 1.0)
+    g.wait_ge(M.lsp, 16)
+    g.partition_broadcast(T.spb[:], T.spi[0:1, :], 128).then_inc(M.gc2, 1)
+    g.wait_ge(M.v, n["v"])
+    g.affine_select(T.vals[:], T.ones[:], [[0, 256]], A.is_ge, 0.0, 16 * (r + 1) - 1, -1).then_inc(M.gc2, 1)
+    iota(M.gc3, T.iv[:], [[0, 2], [32, 3], [1, 16]], 0)
+    iota(M.gc3, T.il16[:], [[1, 16], [0, 2]], 0, False)
+    iota(M.gc3, T.idg[:], [[16, 2], [32, 16]], 0, False)
+    iota(M.gc3, T.itr[:], [[512, 3]], 832)
+    iota(M.gc3, T.rk[:, 0:ZC], [[1, 4], [0, CAPP]], 0)
+    iota(M.gc3, T.rk[:, ZE:FIN], [[1, 4], [0, CAPP]], 4)
+
+    g.vector.wait_ge(M.gc1, 3)
+    V(ts, T.q16[:], T.pidx[:], 15, None, A.bitwise_and)
+    V(ts, T.blk[:], T.pidx[:], 5, None, A.logical_shift_right, dep=False)
+    V(ts, T.half[:], T.pidx[:], 4, 1, A.logical_shift_right, A.bitwise_and, dep=False)
+    V(tc, T.e8[:], T.il8[:], dep=False)
+    V(ms, T.tmp[:, 112:128], 0.0, dep=False)
+    V(ms, T.cmp[:, 256:257], -256.0, dep=False)
+    V(ms, T.cmp[:, 513:514], -256.0, dep=False)
+    g.vector.wait_ge(M.lown, 32)
+    for a in range(4):
+        V(tc, T.ownf[32 * a:32 * a + 32, :], T.owni[0:32, :], dep=not a)
+    V(tc, T.q16f[:], T.q16[:], dep=False)
+    V(tc, T.halff[:], T.half[:], dep=False)
+    V(ts, T.b96[:], T.blk[:], 96.0, None, A.mult, dep=False)
+    V(tc, T.ownu[:], T.ownf[:])
+    V(ts, T.eh[:], T.il8[:], 2.0, T.halff[:], A.mult, A.add, dep=False)
+    V(tt, T.c2[:], T.b96[:], T.q16f[:], A.add, dep=False)
+    V(tc, T.win[:].indirect(T.ownu[:]), T.ones[:])
+    V(ts, T.tt6[:], T.it6[:], T.c2[:], 0.5, A.add, A.add, dep=False)
+    g.vector.wait_ge(M.gc2, 2)
+    V(tc, T.spf[:], T.spb[:])
+    V(ts, T.bt[:], T.tt6[:], -1.0, None, A.mult, dep=False)
+    for j in range(N - 1):
+        V(ts, T.tmp[:, 16 * j:16 * j + 16], T.ownf[:], T.spf[:, j:j + 1], float(CAPP), A.is_ge, A.mult, dep=not j)
+    V(tt, T.tmpb[:], T.tmp[:, 0:64], T.tmp[:, 64:128], A.add)
+    V(tt, T.tmpc[:], T.tmpb[:, 0:32], T.tmpb[:, 32:64], A.add)
+    V(tt, T.basew[:], T.tmpc[:, 0:16], T.tmpc[:, 16:32], A.add)
+    V(tc, T.baseb[:], T.basew[:].indirect(T.eh[:]))
+    V(tp, T.base[:], T.baseb[:])
+
+    g.sync.wait_ge(M.lland, 16)
+    g.sync.wait_ge(M.akey, N - 1)
+    g.sync.dma_start(T.lk[:], T.land[:]).then_inc(M.larr, 16)
+    g.vector.wait_ge(M.larr, 16)
+    V(tc, T.lku[:], T.lk[:])
+    V(tc, T.win[:].indirect(T.lku[:]), T.vals[:])
+    V(tc, T.hb[:], T.win[:].indirect(T.ownu[:]))
+    V(tp, T.xt[:], T.hb[:])
+    V(tt, T.f1[:], T.xt[0:64, 0:256:16], T.xt[64:128, 0:256:16], A.min)
+    V(tt, T.f2[:], T.f1[0:32, :], T.f1[32:64, :], A.min)
+    for a in range(4):
+        V(tt, T.f3[32 * a:32 * a + 32, :], T.f2[:, 0:16:2], T.f2[:, 1:16:2], A.min, dep=not a)
+    V(tc, T.ex[:], T.f3[:].indirect(T.e8[:]))
+    V(tp, T.lin[:], T.ex[:])
+    V(g.vector.tensor_tensor_scan, T.num[:], T.base[:], T.lin[:], 0.0, A.max, A.add)
+    nnum = n["v"]
+    g.scalar.wait_ge(M.v, nnum)
+    for k in range(4):
+        act(T.junk[:, 256 * k:256 * k + 256], T.num[:], AF.Sign, dep=False, bias=T.bt[:, k:k + 1], scale=1.0, accum_out=T.cnt[:, k:k + 1])
+    for k in range(2):
+        V(ts, T.cmp[:, 257 * k:257 * k + 256], T.num[:], T.tt6[:, 4 + k:5 + k], 2.0, A.is_gt, A.mult, dep=not k)
+    for k in range(2):
+        V(red, T.cnt[:, 4 + k:5 + k], T.cmp[:, 257 * k:257 * k + 257], AxisListType.X, A.add, dep=not k)
+    ncnt = n["v"]
+    g.vector.wait_ge(M.s, n["s"])
+    V(ts, T.m6[:], T.cnt[:], -0.5, 128.0, A.mult, A.add)
+    nm6 = n["v"]
+    g.scalar.wait_ge(M.v, ncnt)
+    for x in range(4):
+        o = x + 1 - 2 * (x % 2)
+        act(T.wf[32 * x:32 * x + 32, 6 * o:6 * o + 6], T.cnt[32 * o:32 * o + 32, :], AF.Copy, dep=not x)
+    for x in range(4):
+        V(tc, T.wf[32 * x:32 * x + 32, 6 * x:6 * x + 6], T.cnt[32 * x:32 * x + 32, :], dep=not x)
+    g.vector.wait_ge(M.s, n["s"])
+    for i in range(4):
+        f, to = i // 2, i % 2
+        V(ts, T.wl[64 * to:64 * to + 64, 12 * f:12 * f + 12], T.wf[64 * f:64 * f + 64, 12 * f:12 * f + 12], -0.5, 128.0, A.mult, A.add, dep=not i)
+    nwl = n["v"]
+    g.vector.wait_ge(M.lk, 64)
+    V(tc, T.slot[:].bitcast(dt.uint32), T.kown[:].bitcast(dt.uint32).indirect(T.wl[:]))
+    nslot = n["v"]
+    g.scalar.wait_ge(M.lk, 64)
+    g.scalar.wait_ge(M.v, nwl)
+    act(T.slots[:], T.kowns[:].indirect(T.wl[:]), AF.Copy)
+    nslots = n["s"]
+    for a, b, sa, sx, nm, bc in ((T.slot, T.fin, M.acode, M.xcode, nslot, True), (T.slots, T.fins, M.ascale, M.xscale, nslots, False)):
+        g.wait_ge(M.v if bc else M.s, nm)
+        tr = []
+        for k, d in enumerate(others):
+            x, z = a[:, CAPP * d:CAPP * d + CAPP], b[:, at(r):at(r) + CAPP]
+            if bc:
+                x, z = x.bitcast(dt.uint8), z.bitcast(dt.uint8)
+            tr.append(RemoteDMATransfer(dst_ids=[dst(d)], dma_engine_mask=eng(d, k), remote_sem=sa, src=x, dst=z))
+        g.remote_dma_fused(tr, local_sem=sx)
+    g.sync.wait_ge(M.v, nm6)
+    for a in range(4):
+        g.sync.dma_start(T.land3[r, a:128:4, :], T.m6[32 * a:32 * a + 32, :]).then_inc(M.lmsg, 16)
+    g.wait_ge(M.lmsg, 64)
+    g.remote_dma_fused([RemoteDMATransfer(dst_ids=[dst(d) for d in others], dma_engine_mask=eng(others[0], N - 1), remote_sem=M.amsg,
+                                          srcs=[T.land3[r]], dsts=[T.land3[r] for d in others])], local_sem=M.xmsg)
+
+    V(tc, T.lkf[:], T.lk[:])
+    g.vector.wait_ge(M.gc3, 6)
+    V(tc, T.e16[:], T.il16[:], dep=False)
+    V(ts, T.edg[:], T.idg[:], T.q16f[:], None, A.add, dep=False)
+    V(ms, T.zt[:], 0.0, dep=False)
+    V(tc, T.kx[:], T.lkf[:].indirect(T.e16[:]))
+    V(g.vector.quantize_mx, T.zq[:], T.zqs[:], T.zt[:], dep=False)
+    V(tp, T.kg[:], T.kx[:])
+    nz = n["v"]
+    V(tc, T.kl[:, 0:256], T.kg[:].indirect(T.edg[:, 0:16]))
+    V(tc, T.kl[:, 272:528], T.kg[:].indirect(T.edg[:, 16:32]), dep=False)
+    V(ms, T.kl[:, 256:272], 70000.0, dep=False)
+    V(ms, T.kl[:, 528:544], 70000.0, dep=False)
+    V(ms, T.L[:, 0:576], 0.0, dep=False)
+    V(ms, T.yfin[:, ZC:ZE], 0.0, dep=False)
+    V(ms, T.kf[:, ZC:ZE], -1.0, dep=False)
+    V(ms, T.rk[:, ZC:ZE], -1.0, dep=False)
+    V(ms, T.cmp2[:, FIN:FIN + 1], -256.0, dep=False)
+    V(ms, T.cmp2[:, FIN + 1:FIN + 2], 257.0 - FIN, dep=False)
+    V(ts, T.trash[:], T.itr[:], T.q16f[:], None, A.add, dep=False)
+    V(ts, T.c1[:], T.blk[:], 2.0, 16.0, A.is_ge, A.mult, dep=False)
+    V(ts, T.c4[:], T.halff[:], 16.0, -float(ZC), A.mult, A.add, dep=False)
+    V(tt, T.c3[:], T.b96[:], T.c1[:], A.add)
+    V(tt, T.c5[:], T.c3[:], T.c4[:], A.add)
+    V(ts, T.vals2[:], T.iv[:], T.c5[:], None, A.add)
+    g.vector.wait_ge(M.lw, 16)
+    V(g.vector.quantize_mx, T.wq[:], T.wqs[:], T.wt[:], dep=False)
+    nwq = n["v"]
+    g.sync.wait_ge(M.v, nslot)
+    g.sync.dma_start(T.fin[:, at(r):at(r) + CAPP].bitcast(dt.uint8), T.slot[:, CAPP * r:CAPP * r + CAPP].bitcast(dt.uint8)).then_inc(M.lfin, 16)
+    g.sync.wait_ge(M.s, nslots)
+    g.sync.dma_start(T.fins[:, at(r):at(r) + CAPP], T.slots[:, CAPP * r:CAPP * r + CAPP]).then_inc(M.lfin, 16)
+    g.sync.wait_ge(M.v, nz)
+    g.sync.dma_start(T.fin[:, ZC:ZE].bitcast(dt.uint8), T.zq[:, 0:16].bitcast(dt.uint8)).then_inc(M.lzero, 16)
+    g.sync.dma_start(T.fins[:, ZC:ZE], T.zqs[:, 0:16]).then_inc(M.lzero, 16)
+    g.sync.wait_ge(M.lmsg, 64)
+    g.sync.wait_ge(M.amsg, N - 1)
+    for h in range(2):
+        g.sync.dma_start(T.ix[:, 4 * h:4 * h + 3], T.land3[h:N:2, r // 2:128:4, 3 * (r % 2):3 * (r % 2) + 3]).then_inc(M.lix, 16)
+
+    g.vector.wait_ge(M.lix, 32)
+    V(tc, T.k96[:, 0:48], T.kl[:, 0:272].indirect(T.ix[:, 0:3]))
+    V(tc, T.k96[:, 48:96], T.kl[:, 272:544].indirect(T.ix[:, 4:7]), dep=False)
+    nk = n["v"]
+    g.scalar.wait_ge(M.v, nk)
+    for x in range(4):
+        o = x + 1 - 2 * (x % 2)
+        act(T.kf[32 * x:32 * x + 32, at(2 * o):at(2 * o) + 96], T.k96[32 * o:32 * o + 32, :], AF.Copy, dep=not x)
+    for x in range(4):
+        V(tc, T.kf[32 * x:32 * x + 32, at(2 * x):at(2 * x) + 96], T.k96[32 * x:32 * x + 32, :], dep=not x)
+    V(tp, T.kt[:], T.k96[:], dep=False)
+    nkt = n["v"]
+    ns = n["s"]
+    g.vector.wait_ge(M.s, ns)
+    V(tc, T.kf[64:128, 0:ZC], T.kf[0:64, 0:ZC])
+    nkf = n["v"]
+    g.scalar.wait_ge(M.v, nkt)
+    act(T.kf[0:64, ZE:FIN], T.kf[64:128, ZE:FIN], AF.Copy)
+    g.scalar.wait_ge(M.v, nkf)
+    for k in range(2):
+        act(T.junk2[:, FIN * k:FIN * k + FIN], T.kf[:], AF.Sign, dep=not k, bias=T.kt[:, 32 * k:32 * k + 1], scale=-1.0, accum_out=T.s2[:, k:k + 1])
+    ns2 = n["s"]
+    g.vector.wait_ge(M.s, ns + 1)
+    V(ts, T.cmp2[:, 0:FIN], T.kf[:], T.kt[:, 64:65], 2.0, A.is_lt, A.mult)
+    V(red, T.s2[:, 2:3], T.cmp2[:], AxisListType.X, A.add)
+    hi = T.spf[:, r:r + 1] if r < N - 1 else 65536.0
+    V(ts, T.inv[:], T.kt[:, 0:96:32], hi, None, A.is_ge, dep=False)
+    V(tt, T.tr[:], T.inv[:], T.trash[:], A.mult)
+    g.vector.wait_ge(M.s, ns2)
+    V(ts, T.hi[:], T.s2[:], 1 / 32, (FIN - 48) / 32, A.mult, A.add)
+    V(ts, T.pos[:], T.s2[:], 0.5, (FIN - 33) / 2, A.mult, A.add, dep=False)
+    V(ts, T.h16[:], T.hi[:], 16.0, None, A.mult)
+    V(ts, T.h32[:], T.hi[:], 16.0, 16.0, A.mult, A.add, dep=False)
+    for k in range(6):
+        c = k % 3
+        V(ts, T.ou[:, k:k + 1], T.pos[:, c:c + 1], T.tr[:, c:c + 1], (T.h32 if k > 2 else T.h16)[:, c:c + 1], A.max, A.add, dep=not k)
+    V(tc, T.L[:].indirect(T.ou[:]), T.vals2[:])
+    V(tp, T.LT[:], T.L[:, 0:576])
+    V(tt, T.g1[:], T.LT[0:64, 0:576:16], T.LT[64:128, 0:576:16], A.add)
+    V(tt, T.g2[:], T.g1[0:32, :], T.g1[32:64, :], A.add)
+    V(tt, T.g3[:], T.g2[:, 0:36:2], T.g2[:, 1:36:2], A.add)
+    for a in range(4):
+        V(ts, T.ol[32 * a:32 * a + 32, :], T.g3[:], float(ZC), None, A.add, dep=not a)
+    nol = n["v"]
+
+    g.tensor.wait_ge(M.v, nwq)
+    g.tensor.wait_ge(M.lfin, 32)
+    g.tensor.wait_ge(M.acode, N - 1)
+    g.tensor.wait_ge(M.ascale, N - 1)
+    for i, a in enumerate((0, ZE)):
+        if i:
+            g.tensor.wait_ge(M.mm, 1)
+        g.tensor.matmul_mx(T.acc[:, 512 * i:512 * i + ZC], T.wq[:], T.wqs[:], T.fin[:, a:a + ZC], T.fins[:, a:a + ZC], True, True).then_inc(M.mm, 1)
+        g.scalar.wait_ge(M.mm, i + 1)
+        act(T.yfin[:, a:a + ZC], T.acc[:, 512 * i:512 * i + ZC], AF.Copy)
+    ny = n["s"]
+    g.vector.wait_ge(M.lzero, 32)
+    g.vector.wait_ge(M.lfin, 32)
+    g.vector.wait_ge(M.acode, N - 1)
+    V(tc, T.ord[:].bitcast(dt.uint32), T.fin[:].bitcast(dt.uint32).indirect(T.ol[:]))
+    g.sync.wait_ge(M.v, n["v"])
+    g.sync.dma_start(T.oc[:], T.ord[:].bitcast(dt.uint8)).then_inc(M.st, 16)
+    g.vector.wait_ge(M.s, ny)
+    V(tc, T.ysb[:], T.yfin[:].indirect(T.ol[:]))
+    g.scalar.wait_ge(M.v, nol)
+    g.scalar.wait_ge(M.lzero, 32)
+    g.scalar.wait_ge(M.lfin, 32)
+    g.scalar.wait_ge(M.ascale, N - 1)
+    act(T.ords[:], T.fins[:].indirect(T.ol[:]), AF.Copy)
+    g.sync.wait_ge(M.s, n["s"])
+    for k in range(4):
+        g.sync.dma_start(T.osc[4 * k:4 * k + 4, :], T.ords[32 * k:32 * k + 4, :]).then_inc(M.st, 16)
+    g.sync.wait_ge(M.v, n["v"])
+    g.sync.dma_start(T.y[:], T.ysb[:]).then_inc(M.st, 16)
+    for i, (a, b) in enumerate(((T.kf, T.okk), (T.rk, T.okr))):
+        act(b[:], a[:].indirect(T.ol[:]), AF.Copy)
+        g.sync.wait_ge(M.s, n["s"])
+        g.sync.dma_start(T.ok[i:i + 1, :], b[0:1, :]).then_inc(M.st, 16)
+    g.wait_ge(M.xkey, N - 1)
+    g.wait_ge(M.xcode, N - 1)
+    g.wait_ge(M.xscale, N - 1)
+    g.wait_ge(M.xmsg, 1)
+    g.sync.wait_ge(M.st, 16 * 8)

@@ -6,6 +6,8 @@ SLOTS = N * CAPP
 ZC = SLOTS // 2
 ZE = ZC + 16
 FIN = SLOTS + 16
+KW = C + 32
+U = 1 / 128
 
 
 def at(s):
@@ -15,25 +17,27 @@ def at(s):
 F32, BF, I32, U16, CODE, U8 = "float32", "bfloat16", "int32", "uint16", "float8_e4m3fn_x4", "uint8"
 SCRATCH = {
     "land": ("dram", [N, 128, 2], I32),
-    "land3": ("dram", [N, 128, 6], U16),
     "f1": ("sbuf", [64, 16], F32), "f2": ("sbuf", [32, 16], F32),
-    "g1": ("sbuf", [64, 36], F32), "g2": ("sbuf", [32, 36], F32), "g3": ("sbuf", [32, 18], F32),
+    "g1": ("sbuf", [64, 36], F32), "g2": ("sbuf", [32, 36], F32), "g3": ("sbuf", [64, 18], F32),
+    "spi": ("sbuf", [16, 1], I32), "spc": ("sbuf", [16, 1], F32),
     "acc": ("psum", [128, 1024], F32),
 }
-for _d, _l in ((I32, "lk 16, owni 16, spi 16, spb 16, pidx 1, q16 1, blk 1, half 1, il8 16, il16 32, idg 32, hi 3"),
-               (U16, "lku 16, ownu 16, e8 16, eh 16, e16 32, edg 32, wl 24, m6 6, ix 8, ou 6, ol 18"),
-               (BF, "win 65536, ones 256, vals 256, vals2 96, hb 256, xt 256, f3 8, ex 256, lin 256, junk 1024, cmp 514, zt 512, "
-                    "wt 512, junk2 800, cmp2 402, L 2400, LT 576"),
-               (F32, "lkf 16, ownf 16, spf 16, q16f 1, halff 1, b96 1, c1 1, c2 1, c3 1, c4 1, c5 1, it6 6, bt 6, tt6 6, itr 3, "
-                     "trash 3, iv 96, rk 400, tmp 128, tmpb 64, tmpc 32, basew 16, baseb 256, base 256, num 256, cnt 6, wf 24, "
-                     "kx 512, kg 512, kl 544, k96 96, kt 96, kf 400, inv 3, tr 3, s2 3, pos 3, h16 3, h32 3, okk 288, okr 288, "
+for _d, _l in ((I32, "lk 16, lk2 32, owni 16, pidx 1, q16 1, blk 1, half 1, b0 2, hi 3"),
+               (U16, "lku 16, ownu 16, e8 16, eh 16, ek 32, ea 2, ep 2, wl 24, ixa 16, ou 4, ol 18"),
+               (BF, "win 65536, ones 32, unit 256, vals 256, vals2 48, hb 256, xt 256, f3 8, ex 256, lin 256, junk 768, cmp 258, zt 512, "
+                    "wt 512, junk2 800, cmp2 402, L 2400, LT 576, io2 128, base 256, num 256"),
+               (F32, "lkf 48, ownf 16, q16f 1, halff 1, blkf 1, low 1, c1 1, c2 1, c3 1, c4 1, c5 1, c6 1, c7 1, c8 1, c9 1, il2 16, il4 8, "
+                     "it3 3, th 3, itr 3, trash 3, iv 48, rk 400, spx 32, spw 64, pv 16, ox 256, olin 256, s3 2, x2 2, b64 2, "
+                     "off 6, cnt 6, msg 24, ix 32, kx 512, kl 576, kt 96, kf 400, inv 3, tr 3, s2 3, pos 3, h16 3, okg 288, "
                      "yfin 400, ysb 288"),
                (CODE, "kown 272, slot 384, fin 400, ord 288, wq 128, zq 128"),
                (U8, "kowns 272, slots 384, fins 400, ords 288, wqs 128, zqs 128")):
     for _e in _l.split(", "):
         SCRATCH[_e.split(" ")[0]] = ("sbuf", [128, int(_e.split(" ")[1])], _d)
-SEMAPHORES = ["v", "s", "gc1", "gc2", "gc3", "mm", "lland", "lown", "lsp", "lk", "lw", "larr", "lmsg", "lix", "lfin", "lzero",
-              "st", "akey", "acode", "ascale", "amsg", "xkey", "xcode", "xscale", "xmsg"]
+SEMAPHORES = ["v", "s", "gc0", "gc1", "gc2", "mm", "lland", "lown", "lsp", "lk", "lw", "larr", "larr2", "lfin", "lzero",
+              "st", "akey", "acode", "ascale", "amsg", "xkey", "xcode", "xscale", "xmsg",
+              "vown", "volin", "vz", "vnum0", "vnum1", "vlkf", "vmsg", "vwl", "vslot", "vwq", "vk", "vk1", "vk2", "vol", "vord", "vords",
+              "sox", "ss3", "scnt", "skx0", "skx1", "sslots", "sk1", "sk2", "ss2", "sy"]
 
 
 def rank_program(g, core, T, topo):
@@ -42,240 +46,242 @@ def rank_program(g, core, T, topo):
         return
     M = T.sem
     others = [d for d in range(N) if d != r]
-    n = {"v": 0, "s": 0}
+    n, due = {}, {"v": [], "s": []}
 
-    def V(call, *a, dep=True):
-        if dep and n["v"]:
-            g.vector.wait_ge(M.v, n["v"])
-        call(*a).then_inc(M.v, 1)
-        n["v"] += 1
+    def issue(q, queue, call, a, k, dep, to):
+        if dep:
+            for x in due[q]:
+                queue.wait_ge(M[x], n[x])
+            due[q].clear()
+        call(*a, **k).then_inc(M[to], 1)
+        n[to] = n.get(to, 0) + 1
+        if to not in due[q]:
+            due[q].append(to)
 
-    def act(*a, dep=True, **k):
-        if dep and n["s"]:
-            g.scalar.wait_ge(M.s, n["s"])
-        g.scalar.activation(*a, **k).then_inc(M.s, 1)
-        n["s"] += 1
+    def V(call, *a, dep=True, to="v"):
+        issue("v", g.vector, call, a, {}, dep, to)
+
+    def act(*a, dep=True, to="s", **k):
+        issue("s", g.scalar, g.scalar.activation, a, k, dep, to)
+
+    def wait(queue, x):
+        queue.wait_ge(M[x], n[x])
 
     tc, tt, ts = g.vector.tensor_copy, g.vector.tensor_tensor, g.vector.tensor_scalar
     ms, tp, red = g.vector.memset, g.vector.transpose, g.vector.tensor_reduce
 
-    def dst(d):
-        rid, pid = topo.addr(T.cores[d], core)
-        return DstId(rid=rid, pnc=pid)
+    def blk(b, a, c0=None, c1=None):
+        return b[32 * a:32 * a + 32, c0:c1]
 
-    def eng(d, k):
-        return 1 << topo.engines(core, T.cores[d])[k]
+    def send(pairs, arrived, left):
+        tr = []
+        for k, d in enumerate(others):
+            rid, pid = topo.addr(T.cores[d], core)
+            x, z = pairs(d)
+            tr.append(RemoteDMATransfer(dst_ids=[DstId(rid=rid, pnc=pid)], dma_engine_mask=1 << topo.engines(core, T.cores[d])[k],
+                                        remote_sem=arrived, src=x, dst=z))
+        g.remote_dma_fused(tr, local_sem=left)
 
-    def iota(sem, out, pattern, base, f=True):
-        if f:
-            g.iota(out, pattern, base, 0, allow_small_or_imprecise_dtypes=True).then_inc(sem, 1)
-        else:
-            g.iota(out, pattern, base, 0).then_inc(sem, 1)
+    def iota(sem, out, pattern, base):
+        g.iota(out, pattern, base, 0, allow_small_or_imprecise_dtypes=True).then_inc(sem, 1)
 
     g.sync.dma_start(T.land[r], T.ky[:]).then_inc(M.lland, 16)
     for h in range(2):
         g.scalar.dma_start(T.owni[16 * h:16 * h + 16, :], T.ky[:]).then_inc(M.lown, 16)
-    g.sync.dma_start(T.spi[0:1, :], T.sp[:]).then_inc(M.lsp, 16)
+    g.sync.dma_start(T.spi[:], T.sp[:]).then_inc(M.lsp, 16)
     for a, b in ((0, C), (C, 272)):
-        g.scalar.dma_start(T.kown[:, a:b].bitcast(dt.uint8), T.kc[:, 0:4 * (b - a)]).then_inc(M.lk, 16)
-        g.scalar.dma_start(T.kowns[:, a:b], T.ks[:, 0:b - a]).then_inc(M.lk, 16)
-    g.scalar.dma_start(T.wt[:], T.w[:]).then_inc(M.lw, 16)
+        g.sync.dma_start(T.kown[:, a:b].bitcast(dt.uint8), T.kc[:, 0:4 * (b - a)]).then_inc(M.lk, 16)
+        g.sync.dma_start(T.kowns[:, a:b], T.ks[:, 0:b - a]).then_inc(M.lk, 16)
+    g.sync.dma_start(T.wt[:], T.w[:]).then_inc(M.lw, 16)
 
-    g.iota(T.pidx[:], [[0, 1]], 0, 1).then_inc(M.gc1, 1)
-    iota(M.gc1, T.il8[:], [[1, 8], [0, 2]], 0, False)
-    iota(M.gc1, T.it6[:], [[16, 6]], 0)
+    g.iota(T.pidx[:], [[0, 1]], 0, 1).then_inc(M.gc0, 1)
+    g.wait_ge(M.gc0, 1)
+    iota(M.gc1, T.il2[:], [[2, 8], [0, 2]], 0)
+    iota(M.gc1, T.it3[:], [[16, 3]], 0)
+    iota(M.gc1, T.il4[:], [[64, 4], [0, 2]], 0)
+    iota(M.gc1, T.io2[:], [[2, 128]], -256)
     g.wait_ge(M.lland, 16)
-    g.remote_dma_fused([RemoteDMATransfer(dst_ids=[dst(d)], dma_engine_mask=eng(d, k), remote_sem=M.akey,
-                                          src=T.land[r], dst=T.land[r]) for k, d in enumerate(others)], local_sem=M.xkey)
-    V(ms, T.ones[:], 1.0)
-    g.wait_ge(M.lsp, 16)
-    g.partition_broadcast(T.spb[:], T.spi[0:1, :], 128).then_inc(M.gc2, 1)
-    g.wait_ge(M.v, n["v"])
-    g.affine_select(T.vals[:], T.ones[:], [[0, 256]], A.is_ge, 0.0, 16 * (r + 1) - 1, -1).then_inc(M.gc2, 1)
-    iota(M.gc3, T.iv[:], [[0, 2], [32, 3], [1, 16]], 0)
-    iota(M.gc3, T.il16[:], [[1, 16], [0, 2]], 0, False)
-    iota(M.gc3, T.idg[:], [[16, 2], [32, 16]], 0, False)
-    iota(M.gc3, T.itr[:], [[512, 3]], 832)
-    iota(M.gc3, T.rk[:, 0:ZC], [[1, 4], [0, CAPP]], 0)
-    iota(M.gc3, T.rk[:, ZE:FIN], [[1, 4], [0, CAPP]], 4)
+    send(lambda d: (T.land[r], T.land[r]), M.akey, M.xkey)
+    iota(M.gc2, T.iv[:], [[32, 3], [1, 16]], 0)
+    iota(M.gc2, T.itr[:], [[512, 3]], 832)
+    iota(M.gc2, T.rk[:, 0:ZC], [[1, 4], [0, CAPP]], 0)
+    iota(M.gc2, T.rk[:, ZE:FIN], [[1, 4], [0, CAPP]], 4)
 
-    g.vector.wait_ge(M.gc1, 3)
-    V(ts, T.q16[:], T.pidx[:], 15, None, A.bitwise_and)
+    V(ms, T.unit[:], U)
+    V(ms, T.ones[:], 1.0, dep=False)
+    g.vector.wait_ge(M.gc0, 1)
+    V(ts, T.q16[:], T.pidx[:], 15, None, A.bitwise_and, dep=False)
     V(ts, T.blk[:], T.pidx[:], 5, None, A.logical_shift_right, dep=False)
     V(ts, T.half[:], T.pidx[:], 4, 1, A.logical_shift_right, A.bitwise_and, dep=False)
-    V(tc, T.e8[:], T.il8[:], dep=False)
-    V(ms, T.tmp[:, 112:128], 0.0, dep=False)
-    V(ms, T.cmp[:, 256:257], -256.0, dep=False)
-    V(ms, T.cmp[:, 513:514], -256.0, dep=False)
+    V(ts, T.low[:], T.pidx[:], 16.0 * (r + 1), None, A.is_lt, dep=False)
+    V(ms, T.spx[:], 0.0, dep=False)
+    V(tc, T.halff[:], T.half[:])
+    V(tc, T.q16f[:], T.q16[:], dep=False)
+    V(tc, T.blkf[:], T.blk[:], dep=False)
+    V(ms, T.spw[:, 31:32], 0.0, dep=False)
+    V(ts, T.c1[:], T.q16f[:], 1.0, None, A.min)
+    V(ts, T.c2[:], T.blkf[:], 2.0, 31.0, A.mult, A.add, dep=False)
+    g.vector.wait_ge(M.gc1, 4)
+    V(ts, T.eh[:], T.il2[:], T.halff[:], None, A.add, dep=False, to="vown")
     g.vector.wait_ge(M.lown, 32)
     for a in range(4):
-        V(tc, T.ownf[32 * a:32 * a + 32, :], T.owni[0:32, :], dep=not a)
-    V(tc, T.q16f[:], T.q16[:], dep=False)
-    V(tc, T.halff[:], T.half[:], dep=False)
-    V(ts, T.b96[:], T.blk[:], 96.0, None, A.mult, dep=False)
-    V(tc, T.ownu[:], T.ownf[:])
-    V(ts, T.eh[:], T.il8[:], 2.0, T.halff[:], A.mult, A.add, dep=False)
-    V(tt, T.c2[:], T.b96[:], T.q16f[:], A.add, dep=False)
-    V(tc, T.win[:].indirect(T.ownu[:]), T.ones[:])
-    V(ts, T.tt6[:], T.it6[:], T.c2[:], 0.5, A.add, A.add, dep=False)
-    g.vector.wait_ge(M.gc2, 2)
-    V(tc, T.spf[:], T.spb[:])
-    V(ts, T.bt[:], T.tt6[:], -1.0, None, A.mult, dep=False)
-    for j in range(N - 1):
-        V(ts, T.tmp[:, 16 * j:16 * j + 16], T.ownf[:], T.spf[:, j:j + 1], float(CAPP), A.is_ge, A.mult, dep=not j)
-    V(tt, T.tmpb[:], T.tmp[:, 0:64], T.tmp[:, 64:128], A.add)
-    V(tt, T.tmpc[:], T.tmpb[:, 0:32], T.tmpb[:, 32:64], A.add)
-    V(tt, T.basew[:], T.tmpc[:, 0:16], T.tmpc[:, 16:32], A.add)
-    V(tc, T.baseb[:], T.basew[:].indirect(T.eh[:]))
-    V(tp, T.base[:], T.baseb[:])
+        V(tc, blk(T.ownf, a), T.owni[0:32, :], dep=False, to="vown")
+    wait(g.scalar, "vown")
+    act(T.ox[:], T.ownf[:].indirect(T.eh[:]), AF.Copy, to="sox")
+    g.vector.wait_ge(M.lsp, 16)
+    V(tc, T.spc[:], T.spi[:], dep=False)
+    V(ts, T.ep[:, 0:1], T.c1[:], T.c2[:], None, A.add)
+    V(tc, T.ownu[:], T.ownf[:], dep=False)
+    for a in range(4):
+        V(ts, T.spx[32 * a:32 * a + 16, :], T.ones[0:16, :], T.spc[:], None, A.mult, dep=False)
+    V(tp, T.spw[:, 32:64], T.spx[:])
+    V(ts, T.pv[:], T.spw[:].indirect(T.ep[:, 0:1]), -0.5, None, A.add, to="volin")
+    wait(g.vector, "sox")
+    V(tp, T.olin[:], T.ox[:], dep=False, to="volin")
+    V(tc, T.win[:].indirect(T.ownu[:]), T.unit[:], dep=False)
+    wait(g.scalar, "volin")
+    for u in range(2):
+        act(T.junk[:, 256 * u:256 * u + 256], T.olin[:], AF.Sign, dep=False, to="ss3", bias=T.pv[:, u:u + 1], scale=-1.0, accum_out=T.s3[:, u:u + 1])
+    wait(g.vector, "ss3")
+    V(ts, T.x2[:], T.s3[:], 0.0, 225.0, A.min, A.add, dep=False)
+    V(ts, T.vals[:], T.unit[:], T.low[:], None, A.mult, dep=False)
+    V(ts, T.b0[:], T.x2[:], 1 / 64, None, A.mult)
+    V(ts, T.c3[:], T.halff[:], 17.0, None, A.mult, dep=False)
+    V(ts, T.b64[:], T.b0[:], 64.0, None, A.mult)
+    V(ts, T.c4[:], T.halff[:], -31.0, 32.0, A.mult, A.add, dep=False)
+    for u in range(2):
+        V(ts, T.e8[:, 8 * u:8 * u + 8], T.il4[:], T.b64[:, u:u + 1], 1 / 64, A.add, A.mult, dep=not u)
+        V(ts, T.base[:, 128 * u:128 * u + 128], T.io2[:], T.b64[:, u:u + 1], T.s3[:, u:u + 1], A.add, A.is_ge, dep=False)
+        V(ts, T.off[:, 3 * u:3 * u + 3], T.ones[:, 0:3], T.b64[:, u:u + 1], 128.0 + 2 * KW * (r % 2), A.mult, A.add, dep=False)
+    V(ts, T.c9[:], T.q16f[:], 128.5, None, A.add, dep=False)
+    V(ts, T.ek[:, 0:16], T.il2[:], T.c3[:], None, A.add, dep=False)
+    V(ts, T.ek[:, 16:32], T.il2[:], T.c4[:], None, A.add, dep=False)
+    for b, c in ((T.lk2[:], 0), (T.zt[:], 0.0), (T.msg[:], 0.0), (T.cmp[:, 128:258:129], -128.0)):
+        V(ms, b, c, dep=False)
+    V(ts, T.th[:], T.it3[:], T.c9[:], U, A.add, A.mult)
+    V(g.vector.quantize_mx, T.zq[:], T.zqs[:], T.zt[:], dep=False, to="vz")
+    for b, c in ((T.kl[:, C:KW], 70000.0), (T.kl[:, KW + C:2 * KW], 70000.0), (T.L[:, 0:576], 0.0)):
+        V(ms, b, c, dep=False)
 
     g.sync.wait_ge(M.lland, 16)
     g.sync.wait_ge(M.akey, N - 1)
     g.sync.dma_start(T.lk[:], T.land[:]).then_inc(M.larr, 16)
+    wait(g.sync, "vz")
+    g.sync.dma_start(T.lk2[16:128, 0:16], T.land[0:N - 1]).then_inc(M.larr2, 16)
+    g.sync.dma_start(T.lk2[0:112, 16:32], T.land[1:N]).then_inc(M.larr2, 16)
+    g.sync.dma_start(T.fin[:, ZC:ZE].bitcast(dt.uint8), T.zq[:, 0:16].bitcast(dt.uint8)).then_inc(M.lzero, 16)
+    g.sync.dma_start(T.fins[:, ZC:ZE], T.zqs[:, 0:16]).then_inc(M.lzero, 16)
     g.vector.wait_ge(M.larr, 16)
-    V(tc, T.lku[:], T.lk[:])
+    V(tc, T.lku[:], T.lk[:], dep=False)
     V(tc, T.win[:].indirect(T.lku[:]), T.vals[:])
     V(tc, T.hb[:], T.win[:].indirect(T.ownu[:]))
     V(tp, T.xt[:], T.hb[:])
     V(tt, T.f1[:], T.xt[0:64, 0:256:16], T.xt[64:128, 0:256:16], A.min)
     V(tt, T.f2[:], T.f1[0:32, :], T.f1[32:64, :], A.min)
     for a in range(4):
-        V(tt, T.f3[32 * a:32 * a + 32, :], T.f2[:, 0:16:2], T.f2[:, 1:16:2], A.min, dep=not a)
+        V(tt, blk(T.f3, a), T.f2[:, 0:16:2], T.f2[:, 1:16:2], A.min, dep=not a)
     V(tc, T.ex[:], T.f3[:].indirect(T.e8[:]))
     V(tp, T.lin[:], T.ex[:])
-    V(g.vector.tensor_tensor_scan, T.num[:], T.base[:], T.lin[:], 0.0, A.max, A.add)
-    nnum = n["v"]
-    g.scalar.wait_ge(M.v, nnum)
-    for k in range(4):
-        act(T.junk[:, 256 * k:256 * k + 256], T.num[:], AF.Sign, dep=False, bias=T.bt[:, k:k + 1], scale=1.0, accum_out=T.cnt[:, k:k + 1])
-    for k in range(2):
-        V(ts, T.cmp[:, 257 * k:257 * k + 256], T.num[:], T.tt6[:, 4 + k:5 + k], 2.0, A.is_gt, A.mult, dep=not k)
-    for k in range(2):
-        V(red, T.cnt[:, 4 + k:5 + k], T.cmp[:, 257 * k:257 * k + 257], AxisListType.X, A.add, dep=not k)
-    ncnt = n["v"]
-    g.vector.wait_ge(M.s, n["s"])
-    V(ts, T.m6[:], T.cnt[:], -0.5, 128.0, A.mult, A.add)
-    nm6 = n["v"]
-    g.scalar.wait_ge(M.v, ncnt)
+    for u in range(2):
+        V(g.vector.tensor_tensor_scan, T.num[:, 128 * u:128 * u + 128], T.base[:, 128 * u:128 * u + 128], T.lin[:, 128 * u:128 * u + 128],
+          0.0, A.max, A.add, dep=not u, to="vnum%d" % u)
+    for k in (0, 1, 3, 4):
+        if k % 3 == 0:
+            wait(g.scalar, "vnum%d" % (k // 3))
+        act(T.junk[:, 128 * k:128 * k + 128], T.num[:, 128 * (k // 3):128 * (k // 3) + 128], AF.Sign, dep=k == 0, to="scnt",
+            bias=T.th[:, k % 3:k % 3 + 1], scale=-1.0, accum_out=T.cnt[:, k:k + 1])
+    for u in range(2):
+        V(ts, T.cmp[:, 129 * u:129 * u + 128], T.num[:, 128 * u:128 * u + 128], T.th[:, 2:3], 2.0, A.is_lt, A.mult, dep=not u)
+    for u in range(2):
+        V(red, T.cnt[:, 3 * u + 2:3 * u + 3], T.cmp[:, 129 * u:129 * u + 129], AxisListType.X, A.add, dep=not u)
+    V(tc, T.lkf[:, 0:16], T.lk[:], dep=False, to="vlkf")
+    g.vector.wait_ge(M.larr2, 32)
+    V(tc, T.lkf[:, 16:48], T.lk2[:], dep=False, to="vlkf")
+    wait(g.vector, "scnt")
     for x in range(4):
-        o = x + 1 - 2 * (x % 2)
-        act(T.wf[32 * x:32 * x + 32, 6 * o:6 * o + 6], T.cnt[32 * o:32 * o + 32, :], AF.Copy, dep=not x)
+        V(tt, blk(T.msg, r // 2, 6 * x, 6 * x + 6), blk(T.cnt, x), blk(T.off, x), A.add, dep=not x, to="vmsg")
+    wait(g, "vmsg")
+    send(lambda d: (T.msg[:, 3 * d:3 * d + 3], T.ix[:, 4 * r:4 * r + 3]), M.amsg, M.xmsg)
     for x in range(4):
-        V(tc, T.wf[32 * x:32 * x + 32, 6 * x:6 * x + 6], T.cnt[32 * x:32 * x + 32, :], dep=not x)
-    g.vector.wait_ge(M.s, n["s"])
-    for i in range(4):
-        f, to = i // 2, i % 2
-        V(ts, T.wl[64 * to:64 * to + 64, 12 * f:12 * f + 12], T.wf[64 * f:64 * f + 64, 12 * f:12 * f + 12], -0.5, 128.0, A.mult, A.add, dep=not i)
-    nwl = n["v"]
+        V(ts, blk(T.wl, x), blk(T.msg, r // 2), 0.5, -float(KW * (r % 2)), A.mult, A.add, dep=not x, to="vwl")
     g.vector.wait_ge(M.lk, 64)
-    V(tc, T.slot[:].bitcast(dt.uint32), T.kown[:].bitcast(dt.uint32).indirect(T.wl[:]))
-    nslot = n["v"]
+    V(tc, T.slot[:].bitcast(dt.uint32), T.kown[:].bitcast(dt.uint32).indirect(T.wl[:]), to="vslot")
+    wait(g.scalar, "vlkf")
+    act(T.kx[:, 0:C], T.lkf[:].indirect(T.ek[:, 0:16]), AF.Copy, dep=False, to="skx0")
     g.scalar.wait_ge(M.lk, 64)
-    g.scalar.wait_ge(M.v, nwl)
-    act(T.slots[:], T.kowns[:].indirect(T.wl[:]), AF.Copy)
-    nslots = n["s"]
-    for a, b, sa, sx, nm, bc in ((T.slot, T.fin, M.acode, M.xcode, nslot, True), (T.slots, T.fins, M.ascale, M.xscale, nslots, False)):
-        g.wait_ge(M.v if bc else M.s, nm)
-        tr = []
-        for k, d in enumerate(others):
-            x, z = a[:, CAPP * d:CAPP * d + CAPP], b[:, at(r):at(r) + CAPP]
-            if bc:
-                x, z = x.bitcast(dt.uint8), z.bitcast(dt.uint8)
-            tr.append(RemoteDMATransfer(dst_ids=[dst(d)], dma_engine_mask=eng(d, k), remote_sem=sa, src=x, dst=z))
-        g.remote_dma_fused(tr, local_sem=sx)
-    g.sync.wait_ge(M.v, nm6)
-    for a in range(4):
-        g.sync.dma_start(T.land3[r, a:128:4, :], T.m6[32 * a:32 * a + 32, :]).then_inc(M.lmsg, 16)
-    g.wait_ge(M.lmsg, 64)
-    g.remote_dma_fused([RemoteDMATransfer(dst_ids=[dst(d) for d in others], dma_engine_mask=eng(others[0], N - 1), remote_sem=M.amsg,
-                                          srcs=[T.land3[r]], dsts=[T.land3[r] for d in others])], local_sem=M.xmsg)
-
-    V(tc, T.lkf[:], T.lk[:])
-    g.vector.wait_ge(M.gc3, 6)
-    V(tc, T.e16[:], T.il16[:], dep=False)
-    V(ts, T.edg[:], T.idg[:], T.q16f[:], None, A.add, dep=False)
-    V(ms, T.zt[:], 0.0, dep=False)
-    V(tc, T.kx[:], T.lkf[:].indirect(T.e16[:]))
-    V(g.vector.quantize_mx, T.zq[:], T.zqs[:], T.zt[:], dep=False)
-    V(tp, T.kg[:], T.kx[:])
-    nz = n["v"]
-    V(tc, T.kl[:, 0:256], T.kg[:].indirect(T.edg[:, 0:16]))
-    V(tc, T.kl[:, 272:528], T.kg[:].indirect(T.edg[:, 16:32]), dep=False)
-    V(ms, T.kl[:, 256:272], 70000.0, dep=False)
-    V(ms, T.kl[:, 528:544], 70000.0, dep=False)
-    V(ms, T.L[:, 0:576], 0.0, dep=False)
-    V(ms, T.yfin[:, ZC:ZE], 0.0, dep=False)
-    V(ms, T.kf[:, ZC:ZE], -1.0, dep=False)
-    V(ms, T.rk[:, ZC:ZE], -1.0, dep=False)
-    V(ms, T.cmp2[:, FIN:FIN + 1], -256.0, dep=False)
-    V(ms, T.cmp2[:, FIN + 1:FIN + 2], 257.0 - FIN, dep=False)
-    V(ts, T.trash[:], T.itr[:], T.q16f[:], None, A.add, dep=False)
-    V(ts, T.c1[:], T.blk[:], 2.0, 16.0, A.is_ge, A.mult, dep=False)
-    V(ts, T.c4[:], T.halff[:], 16.0, -float(ZC), A.mult, A.add, dep=False)
-    V(tt, T.c3[:], T.b96[:], T.c1[:], A.add)
-    V(tt, T.c5[:], T.c3[:], T.c4[:], A.add)
-    V(ts, T.vals2[:], T.iv[:], T.c5[:], None, A.add)
-    g.vector.wait_ge(M.lw, 16)
-    V(g.vector.quantize_mx, T.wq[:], T.wqs[:], T.wt[:], dep=False)
-    nwq = n["v"]
-    g.sync.wait_ge(M.v, nslot)
+    wait(g.scalar, "vwl")
+    act(T.slots[:], T.kowns[:].indirect(T.wl[:]), AF.Copy, dep=False, to="sslots")
+    act(T.kx[:, C:2 * C], T.lkf[:].indirect(T.ek[:, 16:32]), AF.Copy, dep=False, to="skx1")
+    wait(g, "vslot")
+    send(lambda d: (T.slot[:, CAPP * d:CAPP * d + CAPP].bitcast(dt.uint8), T.fin[:, at(r):at(r) + CAPP].bitcast(dt.uint8)), M.acode, M.xcode)
+    wait(g, "sslots")
+    send(lambda d: (T.slots[:, CAPP * d:CAPP * d + CAPP], T.fins[:, at(r):at(r) + CAPP]), M.ascale, M.xscale)
+    wait(g.sync, "vslot")
     g.sync.dma_start(T.fin[:, at(r):at(r) + CAPP].bitcast(dt.uint8), T.slot[:, CAPP * r:CAPP * r + CAPP].bitcast(dt.uint8)).then_inc(M.lfin, 16)
-    g.sync.wait_ge(M.s, nslots)
+    wait(g.sync, "sslots")
     g.sync.dma_start(T.fins[:, at(r):at(r) + CAPP], T.slots[:, CAPP * r:CAPP * r + CAPP]).then_inc(M.lfin, 16)
-    g.sync.wait_ge(M.v, nz)
-    g.sync.dma_start(T.fin[:, ZC:ZE].bitcast(dt.uint8), T.zq[:, 0:16].bitcast(dt.uint8)).then_inc(M.lzero, 16)
-    g.sync.dma_start(T.fins[:, ZC:ZE], T.zqs[:, 0:16]).then_inc(M.lzero, 16)
-    g.sync.wait_ge(M.lmsg, 64)
-    g.sync.wait_ge(M.amsg, N - 1)
-    for h in range(2):
-        g.sync.dma_start(T.ix[:, 4 * h:4 * h + 3], T.land3[h:N:2, r // 2:128:4, 3 * (r % 2):3 * (r % 2) + 3]).then_inc(M.lix, 16)
 
-    g.vector.wait_ge(M.lix, 32)
-    V(tc, T.k96[:, 0:48], T.kl[:, 0:272].indirect(T.ix[:, 0:3]))
-    V(tc, T.k96[:, 48:96], T.kl[:, 272:544].indirect(T.ix[:, 4:7]), dep=False)
-    nk = n["v"]
-    g.scalar.wait_ge(M.v, nk)
-    for x in range(4):
-        o = x + 1 - 2 * (x % 2)
-        act(T.kf[32 * x:32 * x + 32, at(2 * o):at(2 * o) + 96], T.k96[32 * o:32 * o + 32, :], AF.Copy, dep=not x)
-    for x in range(4):
-        V(tc, T.kf[32 * x:32 * x + 32, at(2 * x):at(2 * x) + 96], T.k96[32 * x:32 * x + 32, :], dep=not x)
-    V(tp, T.kt[:], T.k96[:], dep=False)
-    nkt = n["v"]
-    ns = n["s"]
-    g.vector.wait_ge(M.s, ns)
-    V(tc, T.kf[64:128, 0:ZC], T.kf[0:64, 0:ZC])
-    nkf = n["v"]
-    g.scalar.wait_ge(M.v, nkt)
-    act(T.kf[0:64, ZE:FIN], T.kf[64:128, ZE:FIN], AF.Copy)
-    g.scalar.wait_ge(M.v, nkf)
+    wait(g.vector, "skx0")
+    V(tp, T.kl[:, 0:C], T.kx[:, 0:C], dep=False)
+    V(tc, blk(T.ix, r // 2, 4 * r, 4 * r + 3), blk(T.msg, r // 2, 3 * r, 3 * r + 3), dep=False)
+    V(ts, T.c5[:], T.q16f[:], 3.0, T.q16f[:], A.is_ge, A.add, dep=False)
+    V(ts, T.c6[:], T.blkf[:], 8.0, None, A.mult, dep=False)
+    V(ts, T.c7[:], T.blkf[:], 2.0, 16.0, A.is_ge, A.mult, dep=False)
+    V(ts, T.c8[:], T.halff[:], 16.0, -float(ZC), A.mult, A.add, dep=False)
+    V(ts, T.ea[:, 0:1], T.c5[:], 6.0, T.c6[:], A.min, A.add)
+    V(ts, T.c1[:], T.blkf[:], 96.0, T.c7[:], A.mult, A.add, dep=False)
+    wait(g.vector, "skx1")
+    V(tp, T.kl[:, KW:KW + C], T.kx[:, C:2 * C], dep=False)
+    V(ms, T.kf[:, ZC:ZE], -1.0, dep=False)
+    g.vector.wait_ge(M.gc2, 4)
+    V(ts, T.vals2[:], T.iv[:], T.c1[:], T.c8[:], A.add, A.add)
+    V(ts, T.trash[:], T.itr[:], T.q16f[:], None, A.add, dep=False)
+    for b, c in ((T.rk[:, ZC:ZE], -1.0), (T.yfin[:, ZC:ZE], 0.0), (T.cmp2[:, FIN:FIN + 1], -256.0), (T.cmp2[:, FIN + 1:FIN + 2], 257.0 - FIN)):
+        V(ms, b, c, dep=False)
+    g.vector.wait_ge(M.lw, 16)
+    V(g.vector.quantize_mx, T.wq[:], T.wqs[:], T.wt[:], dep=False, to="vwq")
+
+    g.vector.wait_ge(M.amsg, N - 1)
+    V(ts, T.ixa[:], T.ix[:].indirect(T.ea[:, 0:1]), 0.5, None, A.mult)
+    V(tc, T.kf[:, 0:96], T.kl[:].indirect(T.ixa[:, 0:6]), to="vk")
+    wait(g.scalar, "vk")
+    for x in (0, 2):
+        act(blk(T.kf, x, 96, ZC), blk(T.kf, x + 1, 0, 96), AF.Copy, dep=False, to="sk1")
+        V(tc, blk(T.kf, x + 1, 96, ZC), blk(T.kf, x, 0, 96), dep=not x, to="vk1")
+    V(tp, T.kt[:], T.kf[:, 0:96], dep=False, to="vk2")
+    wait(g.vector, "sk1")
+    wait(g.vector, "vk1")
+    V(tc, T.kf[64:128, ZE:FIN], T.kf[0:64, 0:ZC], dep=False, to="vk2")
+    wait(g.scalar, "vk1")
+    act(T.kf[0:64, ZE:FIN], T.kf[64:128, 0:ZC], AF.Copy, to="sk2")
+    wait(g.scalar, "vk2")
     for k in range(2):
-        act(T.junk2[:, FIN * k:FIN * k + FIN], T.kf[:], AF.Sign, dep=not k, bias=T.kt[:, 32 * k:32 * k + 1], scale=-1.0, accum_out=T.s2[:, k:k + 1])
-    ns2 = n["s"]
-    g.vector.wait_ge(M.s, ns + 1)
+        act(T.junk2[:, FIN * k:FIN * k + FIN], T.kf[:], AF.Sign, dep=not k, to="ss2", bias=T.kt[:, 32 * k:32 * k + 1], scale=-1.0,
+            accum_out=T.s2[:, k:k + 1])
+    wait(g.vector, "sk2")
     V(ts, T.cmp2[:, 0:FIN], T.kf[:], T.kt[:, 64:65], 2.0, A.is_lt, A.mult)
-    V(red, T.s2[:, 2:3], T.cmp2[:], AxisListType.X, A.add)
-    hi = T.spf[:, r:r + 1] if r < N - 1 else 65536.0
+    hi = T.spw[:, 32 + r:33 + r] if r < N - 1 else 65536.0
     V(ts, T.inv[:], T.kt[:, 0:96:32], hi, None, A.is_ge, dep=False)
-    V(tt, T.tr[:], T.inv[:], T.trash[:], A.mult)
-    g.vector.wait_ge(M.s, ns2)
+    V(red, T.s2[:, 2:3], T.cmp2[:], AxisListType.X, A.add)
+    V(tt, T.tr[:], T.inv[:], T.trash[:], A.mult, dep=False)
+    wait(g.vector, "ss2")
     V(ts, T.hi[:], T.s2[:], 1 / 32, (FIN - 48) / 32, A.mult, A.add)
     V(ts, T.pos[:], T.s2[:], 0.5, (FIN - 33) / 2, A.mult, A.add, dep=False)
     V(ts, T.h16[:], T.hi[:], 16.0, None, A.mult)
-    V(ts, T.h32[:], T.hi[:], 16.0, 16.0, A.mult, A.add, dep=False)
-    for k in range(6):
-        c = k % 3
-        V(ts, T.ou[:, k:k + 1], T.pos[:, c:c + 1], T.tr[:, c:c + 1], (T.h32 if k > 2 else T.h16)[:, c:c + 1], A.max, A.add, dep=not k)
-    V(tc, T.L[:].indirect(T.ou[:]), T.vals2[:])
+    for c in range(3):
+        V(ts, T.ou[:, c:c + 1], T.pos[:, c:c + 1], T.tr[:, c:c + 1], T.h16[:, c:c + 1], A.max, A.add, dep=not c)
+    for h in range(2):
+        V(tc, T.L[:, 16 * h:2400].indirect(T.ou[:, 0:3]), T.vals2[:])
     V(tp, T.LT[:], T.L[:, 0:576])
     V(tt, T.g1[:], T.LT[0:64, 0:576:16], T.LT[64:128, 0:576:16], A.add)
     V(tt, T.g2[:], T.g1[0:32, :], T.g1[32:64, :], A.add)
-    V(tt, T.g3[:], T.g2[:, 0:36:2], T.g2[:, 1:36:2], A.add)
-    for a in range(4):
-        V(ts, T.ol[32 * a:32 * a + 32, :], T.g3[:], float(ZC), None, A.add, dep=not a)
-    nol = n["v"]
+    for a in range(2):
+        V(tt, blk(T.g3, a), T.g2[:, 0:36:2], T.g2[:, 1:36:2], A.add, dep=not a)
+    for a in range(2):
+        V(ts, T.ol[64 * a:64 * a + 64, :], T.g3[:], float(ZC), None, A.add, dep=not a, to="vol")
 
-    g.tensor.wait_ge(M.v, nwq)
+    act(blk(T.rk, 0), blk(T.kf, 0), AF.Copy, dep=False)
+    wait(g.tensor, "vwq")
     g.tensor.wait_ge(M.lfin, 32)
     g.tensor.wait_ge(M.acode, N - 1)
     g.tensor.wait_ge(M.ascale, N - 1)
@@ -284,32 +290,27 @@ def rank_program(g, core, T, topo):
             g.tensor.wait_ge(M.mm, 1)
         g.tensor.matmul_mx(T.acc[:, 512 * i:512 * i + ZC], T.wq[:], T.wqs[:], T.fin[:, a:a + ZC], T.fins[:, a:a + ZC], True, True).then_inc(M.mm, 1)
         g.scalar.wait_ge(M.mm, i + 1)
-        act(T.yfin[:, a:a + ZC], T.acc[:, 512 * i:512 * i + ZC], AF.Copy)
-    ny = n["s"]
+        act(T.yfin[:, a:a + ZC], T.acc[:, 512 * i:512 * i + ZC], AF.Copy, dep=False)
     g.vector.wait_ge(M.lzero, 32)
     g.vector.wait_ge(M.lfin, 32)
     g.vector.wait_ge(M.acode, N - 1)
-    V(tc, T.ord[:].bitcast(dt.uint32), T.fin[:].bitcast(dt.uint32).indirect(T.ol[:]))
-    g.sync.wait_ge(M.v, n["v"])
+    V(tc, T.ord[:].bitcast(dt.uint32), T.fin[:].bitcast(dt.uint32).indirect(T.ol[:]), to="vord")
+    g.vector.wait_ge(M.ascale, N - 1)
+    V(tc, T.ords[:], T.fins[:].indirect(T.ol[:]), dep=False, to="vords")
+    wait(g.scalar, "vol")
+    act(T.ysb[:], T.yfin[:].indirect(T.ol[:]), AF.Copy, to="sy")
+    act(T.okg[:], T.rk[:].indirect(T.ol[:]), AF.Copy, dep=False)
+    wait(g.sync, "vord")
     g.sync.dma_start(T.oc[:], T.ord[:].bitcast(dt.uint8)).then_inc(M.st, 16)
-    g.vector.wait_ge(M.s, ny)
-    V(tc, T.ysb[:], T.yfin[:].indirect(T.ol[:]))
-    g.scalar.wait_ge(M.v, nol)
-    g.scalar.wait_ge(M.lzero, 32)
-    g.scalar.wait_ge(M.lfin, 32)
-    g.scalar.wait_ge(M.ascale, N - 1)
-    act(T.ords[:], T.fins[:].indirect(T.ol[:]), AF.Copy)
-    g.sync.wait_ge(M.s, n["s"])
-    for k in range(4):
-        g.sync.dma_start(T.osc[4 * k:4 * k + 4, :], T.ords[32 * k:32 * k + 4, :]).then_inc(M.st, 16)
-    g.sync.wait_ge(M.v, n["v"])
+    wait(g.sync, "sy")
     g.sync.dma_start(T.y[:], T.ysb[:]).then_inc(M.st, 16)
-    for i, (a, b) in enumerate(((T.kf, T.okk), (T.rk, T.okr))):
-        act(b[:], a[:].indirect(T.ol[:]), AF.Copy)
-        g.sync.wait_ge(M.s, n["s"])
-        g.sync.dma_start(T.ok[i:i + 1, :], b[0:1, :]).then_inc(M.st, 16)
-    g.wait_ge(M.xkey, N - 1)
-    g.wait_ge(M.xcode, N - 1)
-    g.wait_ge(M.xscale, N - 1)
-    g.wait_ge(M.xmsg, 1)
+    wait(g.sync, "vords")
+    wait(g.scalar, "s")
+    for i in range(2):
+        g.scalar.dma_start(T.ok[i:i + 1, :], T.okg[32 * i:32 * i + 1, :]).then_inc(M.st, 16)
+    wait(g.scalar, "vords")
+    for k in range(4):
+        (g.sync if k < 3 else g.scalar).dma_start(T.osc[4 * k:4 * k + 4, :], T.ords[32 * k:32 * k + 4, :]).then_inc(M.st, 16)
+    for x in (M.xkey, M.xcode, M.xscale, M.xmsg):
+        g.wait_ge(x, N - 1)
     g.sync.wait_ge(M.st, 16 * 8)

@@ -6,6 +6,7 @@ SLOTS = N * CAPP
 ZC = SLOTS // 2
 ZE = ZC + 16
 FIN = SLOTS + 16
+KFW = FIN + 15
 KW = C + 32
 U = 1 / 128
 
@@ -25,19 +26,20 @@ SCRATCH = {
 for _d, _l in ((I32, "lk 16, lk2 32, owni 16, pidx 1, q16 1, blk 1, half 1, b0 2, hi 3"),
                (U16, "lku 16, ownu 16, e8 16, eh 16, ek 32, ea 2, ep 2, wl 24, ixa 16, ou 4, ol 18"),
                (BF, "win 65536, ones 32, unit 256, vals 256, vals2 48, hb 256, xt 256, f3 8, ex 256, lin 256, junk 768, cmp 258, zt 512, "
-                    "wt 512, junk2 800, cmp2 402, L 2400, LT 576, io2 128, base 256, num 256"),
-               (F32, "lkf 48, ownf 16, q16f 1, halff 1, blkf 1, low 1, c1 1, c2 1, c3 1, c4 1, c5 1, c6 1, c7 1, c8 1, c9 1, il2 16, il4 8, "
-                     "it3 3, th 3, itr 3, trash 3, iv 48, rk 400, spx 32, spw 64, pv 16, ox 256, olin 256, s3 2, x2 2, b64 2, "
-                     "off 6, cnt 6, msg 24, ix 32, kx 512, kl 576, kt 96, kf 400, inv 3, tr 3, s2 3, pos 3, h16 3, okg 288, "
+                    "wt 512, junk2 830, cmp2 417, L 2400, LT 576, io2 128, base 256, num 256"),
+               (F32, "lkf 48, ownf 16, q16f 1, halff 1, blkf 1, low 1, c1 1, c2 1, c3 1, c4 1, c5 1, c6 1, c7 1, c8 1, c9 1, c10 1, c11 1, "
+                     "q32 1, il2 16, il4 8, it3 3, th 3, itr 3, trash 3, iv 48, rk 400, spx 32, spw 64, pv 16, ox 256, olin 288, s3 2, "
+                     "b64 2, off 6, cnt 6, msg 24, ix 32, kx 512, kl 576, kt 96, kf 415, inv 3, tr 3, s2 3, pos 3, okg 288, "
                      "yfin 400, ysb 288"),
                (CODE, "kown 272, slot 384, fin 400, ord 288, wq 128, zq 128"),
                (U8, "kowns 272, slots 384, fins 400, ords 288, wqs 128, zqs 128")):
     for _e in _l.split(", "):
         SCRATCH[_e.split(" ")[0]] = ("sbuf", [128, int(_e.split(" ")[1])], _d)
-SEMAPHORES = ["v", "s", "gc0", "gc1", "gc2", "mm", "lland", "lown", "lsp", "lk", "lw", "larr", "larr2", "lfin", "lzero",
+SEMAPHORES = ["v", "s", "gc0", "gc1", "gc2", "gc3", "mm", "lland", "lown", "lsp", "lk", "lw", "larr", "larr2", "lfin", "lzero",
               "st", "akey", "acode", "ascale", "amsg", "xkey", "xcode", "xscale", "xmsg",
-              "vown", "volin", "vz", "vnum0", "vnum1", "vlkf", "vmsg", "vwl", "vslot", "vwq", "vk", "vk1", "vk2", "vol", "vord", "vords",
-              "sox", "ss3", "scnt", "skx0", "skx1", "sslots", "sk1", "sk2", "ss2", "sy"]
+              "vunit", "vown", "vb64", "volin", "vz", "vnum0", "vnum1", "vlkf", "vmsg", "vwl", "vslot", "vwq", "vk", "vk1", "vk2", "vinv",
+              "vtr", "vol", "vord", "vords",
+              "sox", "sz", "sc1", "sc2", "ss3", "scnt", "skx", "sslots", "sk1", "sk2", "ss2", "sy"]
 
 
 def rank_program(g, core, T, topo):
@@ -48,21 +50,21 @@ def rank_program(g, core, T, topo):
     others = [d for d in range(N) if d != r]
     n, due = {}, {"v": [], "s": []}
 
-    def issue(q, queue, call, a, k, dep, to):
+    def issue(q, queue, call, a, k, dep, to, aside):
         if dep:
             for x in due[q]:
                 queue.wait_ge(M[x], n[x])
             due[q].clear()
         call(*a, **k).then_inc(M[to], 1)
         n[to] = n.get(to, 0) + 1
-        if to not in due[q]:
+        if to not in due[q] and not aside:
             due[q].append(to)
 
-    def V(call, *a, dep=True, to="v"):
-        issue("v", g.vector, call, a, {}, dep, to)
+    def V(call, *a, dep=True, to="v", aside=False):
+        issue("v", g.vector, call, a, {}, dep, to, aside)
 
     def act(*a, dep=True, to="s", **k):
-        issue("s", g.scalar, g.scalar.activation, a, k, dep, to)
+        issue("s", g.scalar, g.scalar.activation, a, k, dep, to, False)
 
     def wait(queue, x):
         queue.wait_ge(M[x], n[x])
@@ -85,29 +87,34 @@ def rank_program(g, core, T, topo):
     def iota(sem, out, pattern, base):
         g.iota(out, pattern, base, 0, allow_small_or_imprecise_dtypes=True).then_inc(sem, 1)
 
+    def lin(out, x, scale, bias, dep=False, to="s"):
+        act(out, x, AF.Identity, dep=dep, to=to, scale=scale, bias=bias)
+
+    def fill(out, k, c, to="s"):
+        act(out, T.unit[:, 0:k], AF.Copy, dep=False, to=to, scale=c / U)
+
     g.sync.dma_start(T.land[r], T.ky[:]).then_inc(M.lland, 16)
     for h in range(2):
         g.scalar.dma_start(T.owni[16 * h:16 * h + 16, :], T.ky[:]).then_inc(M.lown, 16)
     g.sync.dma_start(T.spi[:], T.sp[:]).then_inc(M.lsp, 16)
+    g.sync.dma_start(T.wt[:], T.w[:]).then_inc(M.lw, 16)
     for a, b in ((0, C), (C, 272)):
         g.sync.dma_start(T.kown[:, a:b].bitcast(dt.uint8), T.kc[:, 0:4 * (b - a)]).then_inc(M.lk, 16)
         g.sync.dma_start(T.kowns[:, a:b], T.ks[:, 0:b - a]).then_inc(M.lk, 16)
-    g.sync.dma_start(T.wt[:], T.w[:]).then_inc(M.lw, 16)
 
     g.iota(T.pidx[:], [[0, 1]], 0, 1).then_inc(M.gc0, 1)
-    g.wait_ge(M.gc0, 1)
     iota(M.gc1, T.il2[:], [[2, 8], [0, 2]], 0)
-    iota(M.gc1, T.it3[:], [[16, 3]], 0)
-    iota(M.gc1, T.il4[:], [[64, 4], [0, 2]], 0)
-    iota(M.gc1, T.io2[:], [[2, 128]], -256)
     g.wait_ge(M.lland, 16)
     send(lambda d: (T.land[r], T.land[r]), M.akey, M.xkey)
-    iota(M.gc2, T.iv[:], [[32, 3], [1, 16]], 0)
-    iota(M.gc2, T.itr[:], [[512, 3]], 832)
-    iota(M.gc2, T.rk[:, 0:ZC], [[1, 4], [0, CAPP]], 0)
-    iota(M.gc2, T.rk[:, ZE:FIN], [[1, 4], [0, CAPP]], 4)
+    iota(M.gc2, T.io2[:], [[2, 128]], -KW)
+    iota(M.gc2, T.il4[:], [[64, 4], [0, 2]], 0)
+    iota(M.gc3, T.it3[:], [[16, 3]], 0)
+    iota(M.gc3, T.iv[:], [[32, 3], [1, 16]], 0)
+    iota(M.gc3, T.itr[:], [[1024, 3]], 896)
+    iota(M.gc3, T.rk[:, 0:ZC], [[1, 4], [0, CAPP]], 0)
+    iota(M.gc3, T.rk[:, ZE:FIN], [[1, 4], [0, CAPP]], 4)
 
-    V(ms, T.unit[:], U)
+    V(ms, T.unit[:], U, to="vunit")
     V(ms, T.ones[:], 1.0, dep=False)
     g.vector.wait_ge(M.gc0, 1)
     V(ts, T.q16[:], T.pidx[:], 15, None, A.bitwise_and, dep=False)
@@ -115,53 +122,81 @@ def rank_program(g, core, T, topo):
     V(ts, T.half[:], T.pidx[:], 4, 1, A.logical_shift_right, A.bitwise_and, dep=False)
     V(ts, T.low[:], T.pidx[:], 16.0 * (r + 1), None, A.is_lt, dep=False)
     V(ms, T.spx[:], 0.0, dep=False)
+    V(ms, T.spw[:, 31:32], 0.0, dep=False)
+    V(ms, T.lk2[:], 0, dep=False)
     V(tc, T.halff[:], T.half[:])
+    V(ts, T.c1[:], T.q16[:], 1.0, None, A.min, dep=False)
+    V(ts, T.c2[:], T.blk[:], 2.0, 31.0, A.mult, A.add, dep=False)
     V(tc, T.q16f[:], T.q16[:], dep=False)
     V(tc, T.blkf[:], T.blk[:], dep=False)
-    V(ms, T.spw[:, 31:32], 0.0, dep=False)
-    V(ts, T.c1[:], T.q16f[:], 1.0, None, A.min)
-    V(ts, T.c2[:], T.blkf[:], 2.0, 31.0, A.mult, A.add, dep=False)
-    g.vector.wait_ge(M.gc1, 4)
-    V(ts, T.eh[:], T.il2[:], T.halff[:], None, A.add, dep=False, to="vown")
+    V(ts, T.c7[:], T.blk[:], 2.0, 16.0, A.is_ge, A.mult, dep=False)
+    g.vector.wait_ge(M.gc1, 1)
+    V(ts, T.eh[:], T.il2[:], T.halff[:], None, A.add, to="vown")
+    V(ts, T.ep[:, 0:1], T.c1[:], T.c2[:], None, A.add, dep=False)
+    wait(g.scalar, "vunit")
+    fill(T.olin[:, C:KW], KW - C, 70000.0, to="sox")
+    for h in range(2):
+        fill(T.zt[:, C * h:C * h + C], C, 0.0, to="sz")
     g.vector.wait_ge(M.lown, 32)
     for a in range(4):
         V(tc, blk(T.ownf, a), T.owni[0:32, :], dep=False, to="vown")
     wait(g.scalar, "vown")
-    act(T.ox[:], T.ownf[:].indirect(T.eh[:]), AF.Copy, to="sox")
+    act(T.ox[:], T.ownf[:].indirect(T.eh[:]), AF.Copy, dep=False, to="sox")
     g.vector.wait_ge(M.lsp, 16)
     V(tc, T.spc[:], T.spi[:], dep=False)
-    V(ts, T.ep[:, 0:1], T.c1[:], T.c2[:], None, A.add)
-    V(tc, T.ownu[:], T.ownf[:], dep=False)
     for a in range(4):
-        V(ts, T.spx[32 * a:32 * a + 16, :], T.ones[0:16, :], T.spc[:], None, A.mult, dep=False)
+        V(ts, T.spx[32 * a:32 * a + 16, :], T.ones[0:16, :], T.spc[:], None, A.mult, dep=not a)
+    V(tc, T.ownu[:], T.ownf[:], dep=False)
     V(tp, T.spw[:, 32:64], T.spx[:])
     V(ts, T.pv[:], T.spw[:].indirect(T.ep[:, 0:1]), -0.5, None, A.add, to="volin")
     wait(g.vector, "sox")
-    V(tp, T.olin[:], T.ox[:], dep=False, to="volin")
+    V(tp, T.olin[:, 0:C], T.ox[:], dep=False, to="volin")
     V(tc, T.win[:].indirect(T.ownu[:]), T.unit[:], dep=False)
     wait(g.scalar, "volin")
     for u in range(2):
-        act(T.junk[:, 256 * u:256 * u + 256], T.olin[:], AF.Sign, dep=False, to="ss3", bias=T.pv[:, u:u + 1], scale=-1.0, accum_out=T.s3[:, u:u + 1])
+        act(T.junk[:, KW * u:KW * u + KW], T.olin[:], AF.Sign, dep=False, to="ss3", bias=T.pv[:, u:u + 1], scale=-1.0, accum_out=T.s3[:, u:u + 1])
+    act(T.vals[:], T.unit[:], AF.Copy, dep=False, to="sc1", scale=T.low[:])
+    lin(T.c3[:], T.halff[:], 17.0, 0.0, to="sc1")
+    lin(T.c4[:], T.halff[:], -31.0, 32.0, to="sc1")
+    lin(T.c6[:], T.blkf[:], 8.0, 0.0, to="sc1")
     wait(g.vector, "ss3")
-    V(ts, T.x2[:], T.s3[:], 0.0, 225.0, A.min, A.add, dep=False)
-    V(ts, T.vals[:], T.unit[:], T.low[:], None, A.mult, dep=False)
-    V(ts, T.b0[:], T.x2[:], 1 / 64, None, A.mult)
-    V(ts, T.c3[:], T.halff[:], 17.0, None, A.mult, dep=False)
-    V(ts, T.b64[:], T.b0[:], 64.0, None, A.mult)
-    V(ts, T.c4[:], T.halff[:], -31.0, 32.0, A.mult, A.add, dep=False)
+    V(ts, T.b0[:], T.s3[:], -32.0, 0.996 / 64, A.min, A.mult, dep=False)
+    V(ts, T.c5[:], T.q16f[:], 3.0, T.q16f[:], A.is_ge, A.add, dep=False)
+    V(ts, T.b64[:], T.b0[:], 64.0, 256.0, A.mult, A.add, to="vb64")
+    wait(g.vector, "sz")
+    V(g.vector.quantize_mx, T.zq[:], T.zqs[:], T.zt[:], dep=False, to="vz", aside=True)
+    g.vector.wait_ge(M.gc2, 2)
     for u in range(2):
         V(ts, T.e8[:, 8 * u:8 * u + 8], T.il4[:], T.b64[:, u:u + 1], 1 / 64, A.add, A.mult, dep=not u)
         V(ts, T.base[:, 128 * u:128 * u + 128], T.io2[:], T.b64[:, u:u + 1], T.s3[:, u:u + 1], A.add, A.is_ge, dep=False)
-        V(ts, T.off[:, 3 * u:3 * u + 3], T.ones[:, 0:3], T.b64[:, u:u + 1], 128.0 + 2 * KW * (r % 2), A.mult, A.add, dep=False)
-    V(ts, T.c9[:], T.q16f[:], 128.5, None, A.add, dep=False)
+    wait(g.vector, "sc1")
     V(ts, T.ek[:, 0:16], T.il2[:], T.c3[:], None, A.add, dep=False)
     V(ts, T.ek[:, 16:32], T.il2[:], T.c4[:], None, A.add, dep=False)
-    for b, c in ((T.lk2[:], 0), (T.zt[:], 0.0), (T.msg[:], 0.0), (T.cmp[:, 128:258:129], -128.0)):
-        V(ms, b, c, dep=False)
-    V(ts, T.th[:], T.it3[:], T.c9[:], U, A.add, A.mult)
-    V(g.vector.quantize_mx, T.zq[:], T.zqs[:], T.zt[:], dep=False, to="vz")
-    for b, c in ((T.kl[:, C:KW], 70000.0), (T.kl[:, KW + C:2 * KW], 70000.0), (T.L[:, 0:576], 0.0)):
-        V(ms, b, c, dep=False)
+    V(ts, T.ea[:, 0:1], T.c5[:], 6.0, T.c6[:], A.min, A.add, dep=False)
+    g.vector.wait_ge(M.lw, 16)
+    V(g.vector.quantize_mx, T.wq[:], T.wqs[:], T.wt[:], dep=False, to="vwq", aside=True)
+    fill(T.msg[:], 24, 0.0)
+    fill(T.cmp[:, 128:258:129], 2, -128.0)
+    for u in range(2):
+        fill(T.kl[:, KW * u + C:KW * u + KW], KW - C, 70000.0)
+    for a, b in ((0, 256), (256, 512), (512, 576)):
+        fill(T.L[:, a:b], b - a, 0.0)
+    for b, k, c in ((T.kf[:, ZC:ZE], 16, -1.0), (T.kf[:, FIN:KFW], KFW - FIN, -1.0), (T.yfin[:, ZC:ZE], 16, 0.0),
+                    (T.cmp2[:, KFW:KFW + 1], 1, -256.0), (T.cmp2[:, KFW + 1:KFW + 2], 1, 257.0 - KFW)):
+        fill(b, k, c)
+    lin(T.c9[:], T.q16f[:], U, 128.5 * U)
+    lin(T.c8[:], T.halff[:], 16.0, -float(ZC))
+    lin(T.q32[:], T.q16f[:], 2.0, 0.0)
+    lin(T.c10[:], T.blkf[:], 96.0, T.c7[:])
+    wait(g.scalar, "vb64")
+    for u in range(2):
+        lin(T.off[:, 3 * u:3 * u + 3], T.ones[:, 0:3], T.b64[:, u:u + 1], 128.0 + 2 * KW * (r % 2))
+    g.scalar.wait_ge(M.gc3, 5)
+    lin(T.th[:], T.it3[:], U, T.c9[:], dep=True)
+    lin(T.c11[:], T.c10[:], 1.0, T.c8[:])
+    lin(T.trash[:], T.itr[:], 1.0, T.q32[:])
+    fill(T.rk[:, ZC:ZE], 16, -1.0)
+    lin(T.vals2[:], T.iv[:], 1.0, T.c11[:], dep=True, to="sc2")
 
     g.sync.wait_ge(M.lland, 16)
     g.sync.wait_ge(M.akey, N - 1)
@@ -174,7 +209,13 @@ def rank_program(g, core, T, topo):
     g.vector.wait_ge(M.larr, 16)
     V(tc, T.lku[:], T.lk[:], dep=False)
     V(tc, T.win[:].indirect(T.lku[:]), T.vals[:])
+    V(tc, T.lkf[:, 0:16], T.lk[:], dep=False, to="vlkf", aside=True)
     V(tc, T.hb[:], T.win[:].indirect(T.ownu[:]))
+    g.vector.wait_ge(M.larr2, 32)
+    V(tc, T.lkf[:, 16:48], T.lk2[:], dep=False, to="vlkf", aside=True)
+    wait(g.scalar, "vlkf")
+    for u in range(2):
+        act(T.kx[:, C * u:C * u + C], T.lkf[:].indirect(T.ek[:, 16 * u:16 * u + 16]), AF.Copy, dep=False, to="skx")
     V(tp, T.xt[:], T.hb[:])
     V(tt, T.f1[:], T.xt[0:64, 0:256:16], T.xt[64:128, 0:256:16], A.min)
     V(tt, T.f2[:], T.f1[0:32, :], T.f1[32:64, :], A.min)
@@ -185,18 +226,17 @@ def rank_program(g, core, T, topo):
     for u in range(2):
         V(g.vector.tensor_tensor_scan, T.num[:, 128 * u:128 * u + 128], T.base[:, 128 * u:128 * u + 128], T.lin[:, 128 * u:128 * u + 128],
           0.0, A.max, A.add, dep=not u, to="vnum%d" % u)
+    wait(g.scalar, "sc2")
     for k in (0, 1, 3, 4):
         if k % 3 == 0:
             wait(g.scalar, "vnum%d" % (k // 3))
-        act(T.junk[:, 128 * k:128 * k + 128], T.num[:, 128 * (k // 3):128 * (k // 3) + 128], AF.Sign, dep=k == 0, to="scnt",
+        act(T.junk[:, 128 * k:128 * k + 128], T.num[:, 128 * (k // 3):128 * (k // 3) + 128], AF.Sign, dep=False, to="scnt",
             bias=T.th[:, k % 3:k % 3 + 1], scale=-1.0, accum_out=T.cnt[:, k:k + 1])
+    wait(g.vector, "sc2")
     for u in range(2):
         V(ts, T.cmp[:, 129 * u:129 * u + 128], T.num[:, 128 * u:128 * u + 128], T.th[:, 2:3], 2.0, A.is_lt, A.mult, dep=not u)
     for u in range(2):
         V(red, T.cnt[:, 3 * u + 2:3 * u + 3], T.cmp[:, 129 * u:129 * u + 129], AxisListType.X, A.add, dep=not u)
-    V(tc, T.lkf[:, 0:16], T.lk[:], dep=False, to="vlkf")
-    g.vector.wait_ge(M.larr2, 32)
-    V(tc, T.lkf[:, 16:48], T.lk2[:], dep=False, to="vlkf")
     wait(g.vector, "scnt")
     for x in range(4):
         V(tt, blk(T.msg, r // 2, 6 * x, 6 * x + 6), blk(T.cnt, x), blk(T.off, x), A.add, dep=not x, to="vmsg")
@@ -206,12 +246,9 @@ def rank_program(g, core, T, topo):
         V(ts, blk(T.wl, x), blk(T.msg, r // 2), 0.5, -float(KW * (r % 2)), A.mult, A.add, dep=not x, to="vwl")
     g.vector.wait_ge(M.lk, 64)
     V(tc, T.slot[:].bitcast(dt.uint32), T.kown[:].bitcast(dt.uint32).indirect(T.wl[:]), to="vslot")
-    wait(g.scalar, "vlkf")
-    act(T.kx[:, 0:C], T.lkf[:].indirect(T.ek[:, 0:16]), AF.Copy, dep=False, to="skx0")
     g.scalar.wait_ge(M.lk, 64)
     wait(g.scalar, "vwl")
     act(T.slots[:], T.kowns[:].indirect(T.wl[:]), AF.Copy, dep=False, to="sslots")
-    act(T.kx[:, C:2 * C], T.lkf[:].indirect(T.ek[:, 16:32]), AF.Copy, dep=False, to="skx1")
     wait(g, "vslot")
     send(lambda d: (T.slot[:, CAPP * d:CAPP * d + CAPP].bitcast(dt.uint8), T.fin[:, at(r):at(r) + CAPP].bitcast(dt.uint8)), M.acode, M.xcode)
     wait(g, "sslots")
@@ -221,25 +258,10 @@ def rank_program(g, core, T, topo):
     wait(g.sync, "sslots")
     g.sync.dma_start(T.fins[:, at(r):at(r) + CAPP], T.slots[:, CAPP * r:CAPP * r + CAPP]).then_inc(M.lfin, 16)
 
-    wait(g.vector, "skx0")
-    V(tp, T.kl[:, 0:C], T.kx[:, 0:C], dep=False)
+    wait(g.vector, "skx")
     V(tc, blk(T.ix, r // 2, 4 * r, 4 * r + 3), blk(T.msg, r // 2, 3 * r, 3 * r + 3), dep=False)
-    V(ts, T.c5[:], T.q16f[:], 3.0, T.q16f[:], A.is_ge, A.add, dep=False)
-    V(ts, T.c6[:], T.blkf[:], 8.0, None, A.mult, dep=False)
-    V(ts, T.c7[:], T.blkf[:], 2.0, 16.0, A.is_ge, A.mult, dep=False)
-    V(ts, T.c8[:], T.halff[:], 16.0, -float(ZC), A.mult, A.add, dep=False)
-    V(ts, T.ea[:, 0:1], T.c5[:], 6.0, T.c6[:], A.min, A.add)
-    V(ts, T.c1[:], T.blkf[:], 96.0, T.c7[:], A.mult, A.add, dep=False)
-    wait(g.vector, "skx1")
-    V(tp, T.kl[:, KW:KW + C], T.kx[:, C:2 * C], dep=False)
-    V(ms, T.kf[:, ZC:ZE], -1.0, dep=False)
-    g.vector.wait_ge(M.gc2, 4)
-    V(ts, T.vals2[:], T.iv[:], T.c1[:], T.c8[:], A.add, A.add)
-    V(ts, T.trash[:], T.itr[:], T.q16f[:], None, A.add, dep=False)
-    for b, c in ((T.rk[:, ZC:ZE], -1.0), (T.yfin[:, ZC:ZE], 0.0), (T.cmp2[:, FIN:FIN + 1], -256.0), (T.cmp2[:, FIN + 1:FIN + 2], 257.0 - FIN)):
-        V(ms, b, c, dep=False)
-    g.vector.wait_ge(M.lw, 16)
-    V(g.vector.quantize_mx, T.wq[:], T.wqs[:], T.wt[:], dep=False, to="vwq")
+    for u in range(2):
+        V(tp, T.kl[:, KW * u:KW * u + C], T.kx[:, C * u:C * u + C], dep=False)
 
     g.vector.wait_ge(M.amsg, N - 1)
     V(ts, T.ixa[:], T.ix[:].indirect(T.ea[:, 0:1]), 0.5, None, A.mult)
@@ -256,20 +278,22 @@ def rank_program(g, core, T, topo):
     act(T.kf[0:64, ZE:FIN], T.kf[64:128, 0:ZC], AF.Copy, to="sk2")
     wait(g.scalar, "vk2")
     for k in range(2):
-        act(T.junk2[:, FIN * k:FIN * k + FIN], T.kf[:], AF.Sign, dep=not k, to="ss2", bias=T.kt[:, 32 * k:32 * k + 1], scale=-1.0,
+        act(T.junk2[:, KFW * k:KFW * k + KFW], T.kf[:], AF.Sign, dep=not k, to="ss2", bias=T.kt[:, 32 * k:32 * k + 1], scale=-1.0,
             accum_out=T.s2[:, k:k + 1])
     wait(g.vector, "sk2")
-    V(ts, T.cmp2[:, 0:FIN], T.kf[:], T.kt[:, 64:65], 2.0, A.is_lt, A.mult)
+    V(ts, T.cmp2[:, 0:KFW], T.kf[:], T.kt[:, 64:65], 2.0, A.is_lt, A.mult)
     hi = T.spw[:, 32 + r:33 + r] if r < N - 1 else 65536.0
-    V(ts, T.inv[:], T.kt[:, 0:96:32], hi, None, A.is_ge, dep=False)
+    V(ts, T.inv[:], T.kt[:, 0:96:32], hi, -0.5, A.is_ge, A.add, dep=False, to="vinv", aside=True)
     V(red, T.s2[:, 2:3], T.cmp2[:], AxisListType.X, A.add)
-    V(tt, T.tr[:], T.inv[:], T.trash[:], A.mult, dep=False)
+    wait(g.vector, "vinv")
+    V(tt, T.tr[:], T.inv[:], T.trash[:], A.mult, dep=False, to="vtr", aside=True)
     wait(g.vector, "ss2")
-    V(ts, T.hi[:], T.s2[:], 1 / 32, (FIN - 48) / 32, A.mult, A.add)
-    V(ts, T.pos[:], T.s2[:], 0.5, (FIN - 33) / 2, A.mult, A.add, dep=False)
-    V(ts, T.h16[:], T.hi[:], 16.0, None, A.mult)
+    V(ts, T.hi[:], T.s2[:], 1 / 32, 22 - 7.5 / 16, A.mult, A.add)
+    wait(g.vector, "vtr")
     for c in range(3):
-        V(ts, T.ou[:, c:c + 1], T.pos[:, c:c + 1], T.tr[:, c:c + 1], T.h16[:, c:c + 1], A.max, A.add, dep=not c)
+        V(ts, T.pos[:, c:c + 1], T.s2[:, c:c + 1], 0.5, T.tr[:, c:c + 1], A.mult, A.max, dep=False)
+    for c in range(3):
+        V(ts, T.ou[:, c:c + 1], T.hi[:, c:c + 1], 16.0, T.pos[:, c:c + 1], A.mult, A.add, dep=not c)
     for h in range(2):
         V(tc, T.L[:, 16 * h:2400].indirect(T.ou[:, 0:3]), T.vals2[:])
     V(tp, T.LT[:], T.L[:, 0:576])
@@ -280,7 +304,7 @@ def rank_program(g, core, T, topo):
     for a in range(2):
         V(ts, T.ol[64 * a:64 * a + 64, :], T.g3[:], float(ZC), None, A.add, dep=not a, to="vol")
 
-    act(blk(T.rk, 0), blk(T.kf, 0), AF.Copy, dep=False)
+    act(blk(T.rk, 0), blk(T.kf, 0, 0, FIN), AF.Copy, dep=False)
     wait(g.tensor, "vwq")
     g.tensor.wait_ge(M.lfin, 32)
     g.tensor.wait_ge(M.acode, N - 1)

from concourse.bass import DstId, RemoteDMATransfer
from concourse.mybir import dt, AluOpType as A, AxisListType, ActivationFunctionType as AF

N, C, CAPP, S = 8, 256, 48, 288
SLOTS = N * CAPP
ZC = SLOTS // 2
ZE = ZC + 16
FIN = SLOTS + 16
KFW = FIN + 15
KW = C + 32
U = 1 / 128


def at(s):
    return CAPP * s + (16 if CAPP * s >= ZC else 0)


F32, BF, I32, U16, CODE, U8 = "float32", "bfloat16", "int32", "uint16", "float8_e4m3fn_x4", "uint8"
SCRATCH = {
    "land": ("dram", [N, 128, 2], I32),
    "f1": ("sbuf", [64, 16], F32), "f2": ("sbuf", [32, 16], F32),
    "g1": ("sbuf", [64, 36], F32), "g2": ("sbuf", [32, 36], F32), "g3": ("sbuf", [64, 18], F32),
    "spi": ("sbuf", [16, 1], I32), "spc": ("sbuf", [16, 1], F32),
    "acc": ("psum", [128, 1024], F32),
}
for _d, _l in ((I32, "lk 16, lk2 32, owni 16, pidx 1, q16 1, blk 1, half 1, b0 2, hi 3"),
               (U16, "lku 16, ownu 16, e8 16, eh 16, ek 32, ea 2, ep 2, wl 24, ixa 16, ou 4, ol 18"),
               (BF, "win 65536, ones 32, unit 256, vals 256, vals2 48, hb 256, xt 256, f3 8, ex 256, lin 256, junk 768, cmp 258, zt 512, "
                    "wt 512, junk2 830, cmp2 417, L 2400, LT 576, io2 128, base 256, num 256"),
               (F32, "lkf 48, ownf 16, q16f 1, halff 1, blkf 1, low 1, c1 1, c2 1, c3 1, c4 1, c5 1, c6 1, c7 1, c8 1, c9 1, c10 1, c11 1, "
                     "q32 1, il2 16, il4 8, it3 3, th 3, itr 3, trash 3, iv 48, rk 400, spx 32, spw 64, pv 16, ox 256, olin 288, s3 2, "
                     "b64 2, off 6, cnt 6, msg 24, ix 32, kx 512, kl 576, kt 96, kf 415, inv 3, tr 3, s2 3, pos 3, okg 288, "
                     "yfin 400, ysb 288"),
               (CODE, "kown 272, slot 384, fin 400, ord 288, wq 128, zq 128"),
               (U8, "kowns 272, slots 384, fins 400, ords 288, wqs 128, zqs 128")):
    for _e in _l.split(", "):
        SCRATCH[_e.split(" ")[0]] = ("sbuf", [128, int(_e.split(" ")[1])], _d)
SEMAPHORES = ["v", "s", "gc0", "gc1", "gc2", "gc3", "mm", "lland", "lown", "lsp", "lk", "lw", "larr", "larr2", "lfin", "lzero",
              "st", "akey", "acode", "ascale", "amsg", "xkey", "xcode", "xscale", "xmsg",
              "vunit", "vown", "vb64", "volin", "vz", "vnum0", "vnum1", "vlkf", "vmsg", "vwl", "vslot", "vwq", "vk", "vk1", "vk2", "vinv",
              "vtr", "vol", "vord", "vords",
              "sox", "sz", "sc1", "sc2", "ss3", "scnt", "skx", "sslots", "sk1", "sk2", "ss2", "sy"]


def rank_program(g, core, T, topo):
    r = T.rank_of(core)
    if r is None:
        return
    M = T.sem
    others = [d for d in range(N) if d != r]
    n, due = {}, {"v": [], "s": []}

    def issue(q, queue, call, a, k, dep, to, aside):
        if dep:
            for x in due[q]:
                queue.wait_ge(M[x], n[x])
            due[q].clear()
        call(*a, **k).then_inc(M[to], 1)
        n[to] = n.get(to, 0) + 1
        if to not in due[q] and not aside:
            due[q].append(to)

    def V(call, *a, dep=True, to="v", aside=False):
        issue("v", g.vector, call, a, {}, dep, to, aside)

    def act(*a, dep=True, to="s", **k):
        issue("s", g.scalar, g.scalar.activation, a, k, dep, to, False)

    def wait(queue, x):
        queue.wait_ge(M[x], n[x])

    tc, tt, ts = g.vector.tensor_copy, g.vector.tensor_tensor, g.vector.tensor_scalar
    ms, tp, red = g.vector.memset, g.vector.transpose, g.vector.tensor_reduce

    def blk(b, a, c0=None, c1=None):
        return b[32 * a:32 * a + 32, c0:c1]

    def send(pairs, arrived, left):
        tr = []
        for k, d in enumerate(others):
            rid, pid = topo.addr(T.cores[d], core)
            x, z = pairs(d)
            tr.append(RemoteDMATransfer(dst_ids=[DstId(rid=rid, pnc=pid)], dma_engine_mask=1 << topo.engines(core, T.cores[d])[k],
                                        remote_sem=arrived, src=x, dst=z))
        g.remote_dma_fused(tr, local_sem=left)

    def iota(sem, out, pattern, base):
        g.iota(out, pattern, base, 0, allow_small_or_imprecise_dtypes=True).then_inc(sem, 1)

    def lin(out, x, scale, bias, dep=False, to="s"):
        act(out, x, AF.Identity, dep=dep, to=to, scale=scale, bias=bias)

    def fill(out, k, c, to="s"):
        act(out, T.unit[:, 0:k], AF.Copy, dep=False, to=to, scale=c / U)

    g.sync.dma_start(T.land[r], T.ky[:]).then_inc(M.lland, 16)
    for h in range(2):
        g.scalar.dma_start(T.owni[16 * h:16 * h + 16, :], T.ky[:]).then_inc(M.lown, 16)
    g.sync.dma_start(T.spi[:], T.sp[:]).then_inc(M.lsp, 16)
    g.sync.dma_start(T.wt[:], T.w[:]).then_inc(M.lw, 16)
    for a, b in ((0, C), (C, 272)):
        g.sync.dma_start(T.kown[:, a:b].bitcast(dt.uint8), T.kc[:, 0:4 * (b - a)]).then_inc(M.lk, 16)
        g.sync.dma_start(T.kowns[:, a:b], T.ks[:, 0:b - a]).then_inc(M.lk, 16)

    g.iota(T.pidx[:], [[0, 1]], 0, 1).then_inc(M.gc0, 1)
    iota(M.gc1, T.il2[:], [[2, 8], [0, 2]], 0)
    g.wait_ge(M.lland, 16)
    send(lambda d: (T.land[r], T.land[r]), M.akey, M.xkey)
    iota(M.gc2, T.io2[:], [[2, 128]], -KW)
    iota(M.gc2, T.il4[:], [[64, 4], [0, 2]], 0)
    iota(M.gc3, T.it3[:], [[16, 3]], 0)
    iota(M.gc3, T.iv[:], [[32, 3], [1, 16]], 0)
    iota(M.gc3, T.itr[:], [[1024, 3]], 896)
    iota(M.gc3, T.rk[:, 0:ZC], [[1, 4], [0, CAPP]], 0)
    iota(M.gc3, T.rk[:, ZE:FIN], [[1, 4], [0, CAPP]], 4)

    V(ms, T.unit[:], U, to="vunit")
    V(ms, T.ones[:], 1.0, dep=False)
    g.vector.wait_ge(M.gc0, 1)
    V(ts, T.q16[:], T.pidx[:], 15, None, A.bitwise_and, dep=False)
    V(ts, T.blk[:], T.pidx[:], 5, None, A.logical_shift_right, dep=False)
    V(ts, T.half[:], T.pidx[:], 4, 1, A.logical_shift_right, A.bitwise_and, dep=False)
    V(ts, T.low[:], T.pidx[:], 16.0 * (r + 1), None, A.is_lt, dep=False)
    V(ms, T.spx[:], 0.0, dep=False)
    V(ms, T.spw[:, 31:32], 0.0, dep=False)
    V(ms, T.lk2[:], 0, dep=False)
    V(tc, T.halff[:], T.half[:])
    V(ts, T.c1[:], T.q16[:], 1.0, None, A.min, dep=False)
    V(ts, T.c2[:], T.blk[:], 2.0, 31.0, A.mult, A.add, dep=False)
    V(tc, T.q16f[:], T.q16[:], dep=False)
    V(tc, T.blkf[:], T.blk[:], dep=False)
    V(ts, T.c7[:], T.blk[:], 2.0, 16.0, A.is_ge, A.mult, dep=False)
    g.vector.wait_ge(M.gc1, 1)
    V(ts, T.eh[:], T.il2[:], T.halff[:], None, A.add, to="vown")
    V(ts, T.ep[:, 0:1], T.c1[:], T.c2[:], None, A.add, dep=False)
    wait(g.scalar, "vunit")
    fill(T.olin[:, C:KW], KW - C, 70000.0, to="sox")
    for h in range(2):
        fill(T.zt[:, C * h:C * h + C], C, 0.0, to="sz")
    g.vector.wait_ge(M.lown, 32)
    for a in range(4):
        V(tc, blk(T.ownf, a), T.owni[0:32, :], dep=False, to="vown")
    wait(g.scalar, "vown")
    act(T.ox[:], T.ownf[:].indirect(T.eh[:]), AF.Copy, dep=False, to="sox")
    g.vector.wait_ge(M.lsp, 16)
    V(tc, T.spc[:], T.spi[:], dep=False)
    for a in range(4):
        V(ts, T.spx[32 * a:32 * a + 16, :], T.ones[0:16, :], T.spc[:], None, A.mult, dep=not a)
    V(tc, T.ownu[:], T.ownf[:], dep=False)
    V(tp, T.spw[:, 32:64], T.spx[:])
    V(ts, T.pv[:], T.spw[:].indirect(T.ep[:, 0:1]), -0.5, None, A.add, to="volin")
    wait(g.vector, "sox")
    V(tp, T.olin[:, 0:C], T.ox[:], dep=False, to="volin")
    V(tc, T.win[:].indirect(T.ownu[:]), T.unit[:], dep=False)
    wait(g.scalar, "volin")
    for u in range(2):
        act(T.junk[:, KW * u:KW * u + KW], T.olin[:], AF.Sign, dep=False, to="ss3", bias=T.pv[:, u:u + 1], scale=-1.0, accum_out=T.s3[:, u:u + 1])
    act(T.vals[:], T.unit[:], AF.Copy, dep=False, to="sc1", scale=T.low[:])
    lin(T.c3[:], T.halff[:], 17.0, 0.0, to="sc1")
    lin(T.c4[:], T.halff[:], -31.0, 32.0, to="sc1")
    lin(T.c6[:], T.blkf[:], 8.0, 0.0, to="sc1")
    wait(g.vector, "ss3")
    V(ts, T.b0[:], T.s3[:], -32.0, 0.996 / 64, A.min, A.mult, dep=False)
    V(ts, T.c5[:], T.q16f[:], 3.0, T.q16f[:], A.is_ge, A.add, dep=False)
    V(ts, T.b64[:], T.b0[:], 64.0, 256.0, A.mult, A.add, to="vb64")
    wait(g.vector, "sz")
    V(g.vector.quantize_mx, T.zq[:], T.zqs[:], T.zt[:], dep=False, to="vz", aside=True)
    g.vector.wait_ge(M.gc2, 2)
    for u in range(2):
        V(ts, T.e8[:, 8 * u:8 * u + 8], T.il4[:], T.b64[:, u:u + 1], 1 / 64, A.add, A.mult, dep=not u)
        V(ts, T.base[:, 128 * u:128 * u + 128], T.io2[:], T.b64[:, u:u + 1], T.s3[:, u:u + 1], A.add, A.is_ge, dep=False)
    wait(g.vector, "sc1")
    V(ts, T.ek[:, 0:16], T.il2[:], T.c3[:], None, A.add, dep=False)
    V(ts, T.ek[:, 16:32], T.il2[:], T.c4[:], None, A.add, dep=False)
    V(ts, T.ea[:, 0:1], T.c5[:], 6.0, T.c6[:], A.min, A.add, dep=False)
    g.vector.wait_ge(M.lw, 16)
    V(g.vector.quantize_mx, T.wq[:], T.wqs[:], T.wt[:], dep=False, to="vwq", aside=True)
    fill(T.msg[:], 24, 0.0)
    fill(T.cmp[:, 128:258:129], 2, -128.0)
    for u in range(2):
        fill(T.kl[:, KW * u + C:KW * u + KW], KW - C, 70000.0)
    for a, b in ((0, 256), (256, 512), (512, 576)):
        fill(T.L[:, a:b], b - a, 0.0)
    for b, k, c in ((T.kf[:, ZC:ZE], 16, -1.0), (T.kf[:, FIN:KFW], KFW - FIN, -1.0), (T.yfin[:, ZC:ZE], 16, 0.0),
                    (T.cmp2[:, KFW:KFW + 1], 1, -256.0), (T.cmp2[:, KFW + 1:KFW + 2], 1, 257.0 - KFW)):
        fill(b, k, c)
    lin(T.c9[:], T.q16f[:], U, 128.5 * U)
    lin(T.c8[:], T.halff[:], 16.0, -float(ZC))
    lin(T.q32[:], T.q16f[:], 2.0, 0.0)
    lin(T.c10[:], T.blkf[:], 96.0, T.c7[:])
    wait(g.scalar, "vb64")
    for u in range(2):
        lin(T.off[:, 3 * u:3 * u + 3], T.ones[:, 0:3], T.b64[:, u:u + 1], 128.0 + 2 * KW * (r % 2))
    g.scalar.wait_ge(M.gc3, 5)
    lin(T.th[:], T.it3[:], U, T.c9[:], dep=True)
    lin(T.c11[:], T.c10[:], 1.0, T.c8[:])
    lin(T.trash[:], T.itr[:], 1.0, T.q32[:])
    fill(T.rk[:, ZC:ZE], 16, -1.0)
    lin(T.vals2[:], T.iv[:], 1.0, T.c11[:], dep=True, to="sc2")

    g.sync.wait_ge(M.lland, 16)
    g.sync.wait_ge(M.akey, N - 1)
    g.sync.dma_start(T.lk[:], T.land[:]).then_inc(M.larr, 16)
    wait(g.sync, "vz")
    g.sync.dma_start(T.lk2[16:128, 0:16], T.land[0:N - 1]).then_inc(M.larr2, 16)
    g.sync.dma_start(T.lk2[0:112, 16:32], T.land[1:N]).then_inc(M.larr2, 16)
    g.sync.dma_start(T.fin[:, ZC:ZE].bitcast(dt.uint8), T.zq[:, 0:16].bitcast(dt.uint8)).then_inc(M.lzero, 16)
    g.sync.dma_start(T.fins[:, ZC:ZE], T.zqs[:, 0:16]).then_inc(M.lzero, 16)
    g.vector.wait_ge(M.larr, 16)
    V(tc, T.lku[:], T.lk[:], dep=False)
    V(tc, T.win[:].indirect(T.lku[:]), T.vals[:])
    V(tc, T.lkf[:, 0:16], T.lk[:], dep=False, to="vlkf", aside=True)
    V(tc, T.hb[:], T.win[:].indirect(T.ownu[:]))
    g.vector.wait_ge(M.larr2, 32)
    V(tc, T.lkf[:, 16:48], T.lk2[:], dep=False, to="vlkf", aside=True)
    wait(g.scalar, "vlkf")
    for u in range(2):
        act(T.kx[:, C * u:C * u + C], T.lkf[:].indirect(T.ek[:, 16 * u:16 * u + 16]), AF.Copy, dep=False, to="skx")
    V(tp, T.xt[:], T.hb[:])
    V(tt, T.f1[:], T.xt[0:64, 0:256:16], T.xt[64:128, 0:256:16], A.min)
    V(tt, T.f2[:], T.f1[0:32, :], T.f1[32:64, :], A.min)
    for a in range(4):
        V(tt, blk(T.f3, a), T.f2[:, 0:16:2], T.f2[:, 1:16:2], A.min, dep=not a)
    V(tc, T.ex[:], T.f3[:].indirect(T.e8[:]))
    V(tp, T.lin[:], T.ex[:])
    for u in range(2):
        V(g.vector.tensor_tensor_scan, T.num[:, 128 * u:128 * u + 128], T.base[:, 128 * u:128 * u + 128], T.lin[:, 128 * u:128 * u + 128],
          0.0, A.max, A.add, dep=not u, to="vnum%d" % u)
    wait(g.scalar, "sc2")
    for k in (0, 1, 3, 4):
        if k % 3 == 0:
            wait(g.scalar, "vnum%d" % (k // 3))
        act(T.junk[:, 128 * k:128 * k + 128], T.num[:, 128 * (k // 3):128 * (k // 3) + 128], AF.Sign, dep=False, to="scnt",
            bias=T.th[:, k % 3:k % 3 + 1], scale=-1.0, accum_out=T.cnt[:, k:k + 1])
    wait(g.vector, "sc2")
    for u in range(2):
        V(ts, T.cmp[:, 129 * u:129 * u + 128], T.num[:, 128 * u:128 * u + 128], T.th[:, 2:3], 2.0, A.is_lt, A.mult, dep=not u)
    for u in range(2):
        V(red, T.cnt[:, 3 * u + 2:3 * u + 3], T.cmp[:, 129 * u:129 * u + 129], AxisListType.X, A.add, dep=not u)
    wait(g.vector, "scnt")
    for x in range(4):
        V(tt, blk(T.msg, r // 2, 6 * x, 6 * x + 6), blk(T.cnt, x), blk(T.off, x), A.add, dep=not x, to="vmsg")
    wait(g, "vmsg")
    send(lambda d: (T.msg[:, 3 * d:3 * d + 3], T.ix[:, 4 * r:4 * r + 3]), M.amsg, M.xmsg)
    for x in range(4):
        V(ts, blk(T.wl, x), blk(T.msg, r // 2), 0.5, -float(KW * (r % 2)), A.mult, A.add, dep=not x, to="vwl")
    g.vector.wait_ge(M.lk, 64)
    V(tc, T.slot[:].bitcast(dt.uint32), T.kown[:].bitcast(dt.uint32).indirect(T.wl[:]), to="vslot")
    g.scalar.wait_ge(M.lk, 64)
    wait(g.scalar, "vwl")
    act(T.slots[:], T.kowns[:].indirect(T.wl[:]), AF.Copy, dep=False, to="sslots")
    wait(g, "vslot")
    send(lambda d: (T.slot[:, CAPP * d:CAPP * d + CAPP].bitcast(dt.uint8), T.fin[:, at(r):at(r) + CAPP].bitcast(dt.uint8)), M.acode, M.xcode)
    wait(g, "sslots")
    send(lambda d: (T.slots[:, CAPP * d:CAPP * d + CAPP], T.fins[:, at(r):at(r) + CAPP]), M.ascale, M.xscale)
    wait(g.sync, "vslot")
    g.sync.dma_start(T.fin[:, at(r):at(r) + CAPP].bitcast(dt.uint8), T.slot[:, CAPP * r:CAPP * r + CAPP].bitcast(dt.uint8)).then_inc(M.lfin, 16)
    wait(g.sync, "sslots")
    g.sync.dma_start(T.fins[:, at(r):at(r) + CAPP], T.slots[:, CAPP * r:CAPP * r + CAPP]).then_inc(M.lfin, 16)

    wait(g.vector, "skx")
    V(tc, blk(T.ix, r // 2, 4 * r, 4 * r + 3), blk(T.msg, r // 2, 3 * r, 3 * r + 3), dep=False)
    for u in range(2):
        V(tp, T.kl[:, KW * u:KW * u + C], T.kx[:, C * u:C * u + C], dep=False)

    g.vector.wait_ge(M.amsg, N - 1)
    V(ts, T.ixa[:], T.ix[:].indirect(T.ea[:, 0:1]), 0.5, None, A.mult)
    V(tc, T.kf[:, 0:96], T.kl[:].indirect(T.ixa[:, 0:6]), to="vk")
    wait(g.scalar, "vk")
    for x in (0, 2):
        act(blk(T.kf, x, 96, ZC), blk(T.kf, x + 1, 0, 96), AF.Copy, dep=False, to="sk1")
        V(tc, blk(T.kf, x + 1, 96, ZC), blk(T.kf, x, 0, 96), dep=not x, to="vk1")
    V(tp, T.kt[:], T.kf[:, 0:96], dep=False, to="vk2")
    wait(g.vector, "sk1")
    wait(g.vector, "vk1")
    V(tc, T.kf[64:128, ZE:FIN], T.kf[0:64, 0:ZC], dep=False, to="vk2")
    wait(g.scalar, "vk1")
    act(T.kf[0:64, ZE:FIN], T.kf[64:128, 0:ZC], AF.Copy, to="sk2")
    wait(g.scalar, "vk2")
    for k in range(2):
        act(T.junk2[:, KFW * k:KFW * k + KFW], T.kf[:], AF.Sign, dep=not k, to="ss2", bias=T.kt[:, 32 * k:32 * k + 1], scale=-1.0,
            accum_out=T.s2[:, k:k + 1])
    wait(g.vector, "sk2")
    V(ts, T.cmp2[:, 0:KFW], T.kf[:], T.kt[:, 64:65], 2.0, A.is_lt, A.mult)
    hi = T.spw[:, 32 + r:33 + r] if r < N - 1 else 65536.0
    V(ts, T.inv[:], T.kt[:, 0:96:32], hi, -0.5, A.is_ge, A.add, dep=False, to="vinv", aside=True)
    V(red, T.s2[:, 2:3], T.cmp2[:], AxisListType.X, A.add)
    wait(g.vector, "vinv")
    V(tt, T.tr[:], T.inv[:], T.trash[:], A.mult, dep=False, to="vtr", aside=True)
    wait(g.vector, "ss2")
    V(ts, T.hi[:], T.s2[:], 1 / 32, 22 - 7.5 / 16, A.mult, A.add)
    wait(g.vector, "vtr")
    for c in range(3):
        V(ts, T.pos[:, c:c + 1], T.s2[:, c:c + 1], 0.5, T.tr[:, c:c + 1], A.mult, A.max, dep=False)
    for c in range(3):
        V(ts, T.ou[:, c:c + 1], T.hi[:, c:c + 1], 16.0, T.pos[:, c:c + 1], A.mult, A.add, dep=not c)
    for h in range(2):
        V(tc, T.L[:, 16 * h:2400].indirect(T.ou[:, 0:3]), T.vals2[:])
    V(tp, T.LT[:], T.L[:, 0:576])
    V(tt, T.g1[:], T.LT[0:64, 0:576:16], T.LT[64:128, 0:576:16], A.add)
    V(tt, T.g2[:], T.g1[0:32, :], T.g1[32:64, :], A.add)
    for a in range(2):
        V(tt, blk(T.g3, a), T.g2[:, 0:36:2], T.g2[:, 1:36:2], A.add, dep=not a)
    for a in range(2):
        V(ts, T.ol[64 * a:64 * a + 64, :], T.g3[:], float(ZC), None, A.add, dep=not a, to="vol")

    act(blk(T.rk, 0), blk(T.kf, 0, 0, FIN), AF.Copy, dep=False)
    wait(g.tensor, "vwq")
    g.tensor.wait_ge(M.lfin, 32)
    g.tensor.wait_ge(M.acode, N - 1)
    g.tensor.wait_ge(M.ascale, N - 1)
    for i, a in enumerate((0, ZE)):
        if i:
            g.tensor.wait_ge(M.mm, 1)
        g.tensor.matmul_mx(T.acc[:, 512 * i:512 * i + ZC], T.wq[:], T.wqs[:], T.fin[:, a:a + ZC], T.fins[:, a:a + ZC], True, True).then_inc(M.mm, 1)
        g.scalar.wait_ge(M.mm, i + 1)
        act(T.yfin[:, a:a + ZC], T.acc[:, 512 * i:512 * i + ZC], AF.Copy, dep=False)
    g.vector.wait_ge(M.lzero, 32)
    g.vector.wait_ge(M.lfin, 32)
    g.vector.wait_ge(M.acode, N - 1)
    V(tc, T.ord[:].bitcast(dt.uint32), T.fin[:].bitcast(dt.uint32).indirect(T.ol[:]), to="vord")
    g.vector.wait_ge(M.ascale, N - 1)
    V(tc, T.ords[:], T.fins[:].indirect(T.ol[:]), dep=False, to="vords")
    wait(g.scalar, "vol")
    act(T.ysb[:], T.yfin[:].indirect(T.ol[:]), AF.Copy, to="sy")
    act(T.okg[:], T.rk[:].indirect(T.ol[:]), AF.Copy, dep=False)
    wait(g.sync, "vord")
    g.sync.dma_start(T.oc[:], T.ord[:].bitcast(dt.uint8)).then_inc(M.st, 16)
    wait(g.sync, "sy")
    g.sync.dma_start(T.y[:], T.ysb[:]).then_inc(M.st, 16)
    wait(g.sync, "vords")
    wait(g.scalar, "s")
    for i in range(2):
        g.scalar.dma_start(T.ok[i:i + 1, :], T.okg[32 * i:32 * i + 1, :]).then_inc(M.st, 16)
    wait(g.scalar, "vords")
    for k in range(4):
        (g.sync if k < 3 else g.scalar).dma_start(T.osc[4 * k:4 * k + 4, :], T.ords[32 * k:32 * k + 4, :]).then_inc(M.st, 16)
    for x in (M.xkey, M.xcode, M.xscale, M.xmsg):
        g.wait_ge(x, N - 1)
    g.sync.wait_ge(M.st, 16 * 8)
